import numpy as np, ml_dtypes
CORES = [25,29,65,69,153,157,193,197]
N = 8
BF = ml_dtypes.bfloat16
def gentries(a):
    return np.ascontiguousarray(a.reshape(8, 16, -1).transpose(0, 2, 1)).reshape(8, -1)
def gtable(e):
    e = np.asarray(e); return np.ascontiguousarray(e.reshape(8, -1, 16).transpose(0, 2, 1)).reshape(128, -1).astype(np.int32)
M, B, H, ST = 192, 8, 5, 3
W = M * B
def parts(rng):
    c = np.minimum((W * np.exp2(-5 * rng.random((N, 8, 1, W))) * rng.random((N, 8, 16, W))).astype(np.int64), W - 1)
    a = np.exp2(5 * rng.random((N, 8, 16, 1))); q = rng.choice(np.array([1, 1, 1, 16, 256]), (N, 8, 16, 1))
    l = np.minimum((W * rng.random((N, 8, 16, W)) ** a).astype(np.int64), W - 1) & -q
    gap = np.minimum((W * (0.1 + 0.8 * rng.random((N, 8, 1, M))) * (0.5 + rng.random((N, 8, 16, M)))).astype(np.int64), W - 1)
    return c, l, gap, rng.integers(0, B, (N, 8, M))
def pack(c, l, gap, cur):
    return {"ck": np.ascontiguousarray(c.reshape(N, 128, W)).astype(np.int32), "la": np.ascontiguousarray(l.reshape(N, 128, W)).astype(np.int32),
            "gap": np.ascontiguousarray(gap.reshape(N, 128, M)).astype(np.int32), "cu": np.stack([gtable(a) for a in cur])}
def setup_inputs(rng):
    return pack(*parts(rng))
def setup_inputs_ties(rng):
    c, l, gap, cur = parts(rng); c = c & -64; gap = gap & -64; l = l & -64
    kind = rng.integers(0, 4, (N, 8, 16, 1)); kind[:, :, :4, 0] = np.arange(4)
    few = np.take_along_axis(rng.integers(0, W, (N, 8, 16, 4)), rng.integers(0, kind + 1, (N, 8, 16, W)), 3)
    l[:, ::2] = few[:, ::2]
    gap = np.where((rng.random((N, 8, 1, M)) < 0.25) & (rng.random((N, 8, 16, M)) < 0.2), 0, gap)
    return pack(c, l, gap, cur)
def setup_inputs_alike(rng):
    c, l, gap, cur = parts(rng)
    c[:, ::2] = np.maximum(c[:, ::2, :1], 16); c[:, ::2, :, 0] = rng.integers(0, 16, (N, 4, 16))
    c[:, 1::2] = rng.choice(np.array([3, W // 3, W // 2, W - 1]), (N, 4, 16, W))
    cur[:, :, 0] = 0; gap[:, :, :, 0] = 0
    return pack(c, l, gap, cur)
def setup_inputs_ends(rng):
    c, l, gap, cur = parts(rng)
    c[:, 0:4] = rng.choice(np.array([0, 1, W - 2, W - 1]), (N, 4, 16, W))
    l[:, 2:6] = rng.choice(np.array([0, 1, W - 2, W - 1]), (N, 4, 16, W))
    gap[:, 1:7] = rng.choice(np.array([0, 1, W - 1]), (N, 6, 16, M))
    cur = rng.choice(np.array([0, B - 1]), (N, 8, M))
    return pack(c, l, gap, cur)
def setup_inputs_count(rng):
    c, l, gap, cur = parts(rng); c = np.maximum(c, 1)
    n = rng.choice(np.array([0, H - 1, H, H + 1, 16]), (N, 8, 1, M)); g = rng.permutation(8)
    n[:, g[0]] = 16; n[:, g[1]] = 0; n[:, g[2], 0, :5] = np.array([0, H - 1, H, H + 1, 16])
    cur[:, g[0], :B] = np.arange(B)
    n[0::2, g[3]] = 16; n[1::2, g[3]] = 0
    n[:, g[4]] = 16; l[:, g[4]] = l[:, g[4], :, :1].copy(); c[:, g[4], :, 0] = 0
    cur[:, g[4], 0] = 1; cur[:, g[4], 1:9] = (2 * np.arange(N)[:, None] + np.arange(8)) & (B - 1)
    gap = np.where(np.argsort(rng.random((N, 8, 16, M)), axis=2) < n, 0, W - 1)
    return pack(c, l, gap, cur)
def setup_inputs_spread(rng):
    c, l, gap, cur = parts(rng); e = np.log2(W)
    c = np.minimum((np.exp2(e * rng.random((N, 8, 1, W))) * rng.random((N, 8, 16, W))).astype(np.int64), W - 1)
    l = np.minimum(np.exp2(e * rng.random((N, 8, 16, W)) ** (2 * rng.random((N, 8, 16, 1)))).astype(np.int64), W - 1)
    gap = np.minimum((np.exp2(e * (1 - rng.random((N, 8, 1, M)) ** 3)) * rng.random((N, 8, 16, M))).astype(np.int64), W - 1)
    return pack(c, l, gap, cur)
def check_inputs(d):
    bad = []
    for k, hi in (("ck", W - 1), ("la", W - 1), ("gap", W - 1), ("cu", B - 1)):
        if np.min(d[k]) < 0 or np.max(d[k]) > hi: bad.append("range of " + k)
    return bad
def columns(t, x):
    return np.take_along_axis(t, np.swapaxes(x, 2, 3).reshape(N, 8, 1, 16 * M), 3).reshape(N, 8, 16, M, 16)
def reference(ck, la, gap, cu):
    C = ck.astype(np.int64).reshape(N, 8, 16, W); L = la.astype(np.int64).reshape(N, 8, 16, W); G = gap.astype(np.int64).reshape(N, 8, 16, M)
    cur = np.stack([gentries(a) for a in cu]).astype(np.int64); first = B * np.arange(M)
    I = np.take_along_axis(C, (first + cur)[:, :, None, :], 3); T = I + G
    for step in range(ST):
        A = columns(L, I); top = np.max(A, axis=4, keepdims=True)
        s = np.max(np.where(A < top, A, 0), axis=4)
        I = np.maximum(I, np.max(columns(C, s), axis=4))
        out = np.add.reduce((I >= T).astype(np.int64), axis=2) >= H
        hit = (np.arange(B) == cur[..., None]) & out[..., None]
        C = np.where(hit[:, :, None], I[..., None], C.reshape(N, 8, 16, M, B)).reshape(N, 8, 16, W)
        cur = np.where(out, (cur + 1) & (B - 1), cur)
        new = np.take_along_axis(C, (first + cur)[:, :, None, :], 3)
        T = np.where(out[:, :, None], new + G, T); I = np.where(out[:, :, None], new, I)
        I, T, G, cur = np.roll(I, 1, axis=0), np.roll(T, 1, axis=0), np.roll(G, 1, axis=0), np.roll(cur, 1, axis=0)
    return {"yi": I.reshape(N, 128, M).astype(np.float32), "yc": np.stack([gtable(a) for a in cur]).astype(np.float32)}

@@ -1,0 +1,499 @@
+from concourse.mybir import AluOpType, ActivationFunctionType
+
+M, B, H, ST, W = 192, 8, 5, 3, 1536
+SIZES = [96, 96]
+K = len(SIZES)
+OFF = [sum(SIZES[:k]) for k in range(K)]
+DUMP = M
+BIG = 2048.0
+CB = 4096.0
+HALF = -(H - 0.5) / 16.0
+VL0 = [48, 0]
+VL = [48, 0]
+VG = [0, 0]
+ORDER = """
+0L0 0P0 0V01 0V02 0V00 0S0 0N0 0L1 0P1 0V10 0V11 0G0 0R0 0V12 0Z0 0S1 0F0 0X0 0N1 0G1 0R1 0Z1 0F1 1L0 1P0 0X1 0T
+1V01 1V00 1V02 1N0 1L1 1P1 1S0 1V10 1V11 1V12 1S1 1N1 1G0 1R0 1G1 1R1 1Z0 1F0 1X0 1Z1 1F1 1X1 2L0 2P0 1T
+2V01 2V02 2V00 2N0 2L1 2R0 2P1 2S0 2V10 2G0 2V11 2V12 2S1 2N1 2G1 2Z0 2F0 2R1 2Z1 2X0 2F1 2X1
+""".split()
+
+E = 16 * M
+MW = [2 * n + n // 16 for n in SIZES]
+MO = [sum(MW[:k]) for k in range(K)]
+MT = sum(MW)
+GO = [OFF[k] + OFF[k] // 8 for k in range(K)]
+GW = M + M // 8
+NM = max(SIZES)
+SCRATCH = {
+    "C": ("sbuf", [128, DUMP + W], "int32"),
+    "L": ("sbuf", [128, W], "int32"),
+    "cus": ("sbuf", [128, 12], "int32"),
+    "gaps": ("sbuf", [128, M], "int32"),
+    "GB": ("sbuf", [128, ST * GW], "float16"),
+    "RM": ("sbuf", [128, 16 * NM], "bfloat16"),
+    "EX": ("sbuf", [128, 512], "float16"),
+    "ID": ("sbuf", [128, 128], "float16"),
+    "N4": ("sbuf", [128, 128], "float16"),
+    "NI": ("sbuf", [128, 128], "float16"),
+    "BP": ("sbuf", [128, 128], "float16"),
+    "BN": ("sbuf", [128, 128], "float16"),
+    "HB": ("sbuf", [128, 2 * NM], "float16"),
+    "DM": ("sbuf", [128, M], "float32"),
+    "i1": ("sbuf", [128, 512], "int32"),
+    "i2": ("sbuf", [128, 128], "int32"),
+    "i3": ("sbuf", [128, 128], "int32"),
+    "i4": ("sbuf", [128, M], "int32"),
+    "i5": ("sbuf", [128, 12], "int32"),
+    "i6": ("sbuf", [128, 12], "int32"),
+    "b8": ("sbuf", [128, 12], "float32"),
+    "cd": ("sbuf", [128, 12], "float32"),
+    "I0f": ("sbuf", [128, 12], "float32"),
+    "I0u": ("sbuf", [128, 12], "uint16"),
+    "cuf": ("sbuf", [128, 12], "float16"),
+    "Io0": ("sbuf", [128, M], "float16"),
+    "J0": ("sbuf", [128, M], "uint16"),
+    "wo": ("sbuf", [128, 12 * ST], "float32"),
+    "ou": ("sbuf", [128, 12 * ST], "uint16"),
+    "sg": ("sbuf", [128, 24 * ST], "float16"),
+    "Ru": ("sbuf", [128, 12 * ST], "uint16"),
+    "Ry": ("sbuf", [128, 12], "float32"),
+    "Fy": ("sbuf", [128, 12], "float32"),
+    "oFy": ("sbuf", [128, 12], "float32"),
+    "oFq": ("sbuf", [128, 12], "float32"),
+    "J": ("sbuf", [128, ST * M], "uint16"),
+    "oJ": ("sbuf", [128, ST * M], "uint16"),
+    "Ms": ("sbuf", [128, ST * MT], "float16"),
+    "oMs": ("sbuf", [128, ST * MT], "float16"),
+    "F": ("sbuf", [128, M], "float32"),
+    "oF": ("sbuf", [128, M], "float32"),
+    "tT": ("sbuf", [128, ST * K * 128], "float16"),
+    "xp": ("psum", [128, E], "float32"),
+    "tp": ("psum", [128, 512], "float32"),
+}
+for _n in ("A", "P", "V", "S", "BB", "Z"):
+    SCRATCH[_n] = ("sbuf", [128, ST * E], "float16")
+for _n, _d in (("su", "uint16"), ("RR", "float16"), ("In", "float16"), ("GE", "float16"),
+               ("m1", "float16"), ("DD", "float16"), ("DS", "float16")):
+    SCRATCH[_n] = ("sbuf", [128, ST * M], _d)
+SEMAPHORES = ["v", "a", "p", "gq", "ls", "lcu", "lck0", "lck1", "lla", "lgap", "agap1", "agap2", "aFy", "st"]
+for _k in range(K):
+    for _s in range(1, ST):
+        SEMAPHORES += ["aJ%d_%d" % (_s, _k), "aM%d_%d" % (_s, _k)]
+    SEMAPHORES += ["aF%d" % _k]
+
+MSG = {"agap1": ("GB", GW, 2 * GW, 1), "agap2": ("GB", 2 * GW, 3 * GW, 1), "aFy": ("Fy", 0, 12, 1)}
+for _k in range(K):
+    for _s in range(1, ST):
+        MSG["aJ%d_%d" % (_s, _k)] = ("J", _s * M + OFF[_k], _s * M + OFF[_k] + SIZES[_k], 0)
+        MSG["aM%d_%d" % (_s, _k)] = ("Ms", _s * MT + MO[_k], _s * MT + MO[_k] + MW[_k], 1)
+    MSG["aF%d" % _k] = ("F", OFF[_k], OFF[_k] + SIZES[_k], 0)
+ISSUE = ["agap1", "agap2"]
+for _t in ORDER:
+    if _t[1] == "F":
+        ISSUE.append("aJ%d_%s" % (int(_t[0]) + 1, _t[2]) if int(_t[0]) < ST - 1 else "aF" + _t[2])
+    if _t[1] == "X" and int(_t[0]) < ST - 1:
+        ISSUE.append("aM%d_%s" % (int(_t[0]) + 1, _t[2]))
+ISSUE.append("aFy")
+
+
+def lanes(topo, cores, src, dst):
+    if topo.may_write(src, dst):
+        return [dst, dst]
+    own = [c for c in topo.cores_of(src) if c not in cores and topo.may_write(c, dst)]
+    own.sort(key=lambda c: (topo.die(c) != topo.die(src), c))
+    return [own[0], own[1 % len(own)]]
+
+
+def nbits(m):
+    return bin(m).count("1")
+
+
+def rank_program(g, core, T, topo):
+    cores = list(T.cores)
+    n_ranks = len(cores)
+    sem = T.sem
+    rank = T.rank_of(core)
+
+    def send(dst, src_name, sname, back=0):
+        name, c0, c1 = MSG[sname][:3]
+        rid, pid = topo.addr(dst, core)
+        m = topo.mask(core, dst)
+        g.remote_dma(T[name][:, c0:c1], T[src_name][:, c0 - back:c1 - back], sem[sname], sem.ls, pid, rid, m)
+        return nbits(m)
+
+    if rank is None:
+        total = 0
+        for r in range(n_ranks):
+            src, dst = cores[r], cores[(r + 1) % n_ranks]
+            way = lanes(topo, cores, src, dst)
+            if core not in way:
+                continue
+            for sname in ISSUE:
+                name, c0, c1, lane = MSG[sname]
+                if way[lane] == core:
+                    g.wait_ge(sem[sname], nbits(topo.mask(src, core)))
+                    total += send(dst, name, sname)
+        if total:
+            g.wait_ge(sem.ls, total)
+        return
+
+    nxt, prv = cores[(rank + 1) % n_ranks], cores[(rank - 1) % n_ranks]
+    way = lanes(topo, cores, core, nxt)
+    inway = lanes(topo, cores, prv, core)
+    arrives = [nbits(topo.mask(prv if w == core else w, core)) for w in inway]
+    sent = [0]
+
+    queues = {"v": (g.vector, "v"), "a": (g.scalar, "a"), "p": (g.tensor, "p"), "g": (g, "gq"), "s": (g.sync, "st")}
+    count = {q: 0 for q in queues}
+    seen = {q: {} for q in queues}
+    wrote, readers, banks = {}, {}, {}
+
+    def wait(q, deps):
+        need = {}
+        for s, val in deps:
+            need[s] = max(need.get(s, 0), val)
+        for s in sorted(need):
+            if seen[q].get(s, 0) < need[s]:
+                queues[q][0].wait_ge(sem[s], need[s])
+                seen[q][s] = need[s]
+
+    def op(q, R, Wk, call, bank=()):
+        d = [wrote[k] for k in R if k in wrote]
+        for k in Wk:
+            if k in wrote:
+                d.append(wrote[k])
+            d += readers.get(k, [])
+        for b in bank:
+            d += [t for qq, t in banks.get(b, {}).items() if qq != q]
+        wait(q, d)
+        s = queues[q][1]
+        call().then_inc(sem[s], 1)
+        count[q] += 1
+        tok = (s, count[q])
+        for k in R:
+            readers.setdefault(k, []).append(tok)
+        for k in Wk:
+            wrote[k] = tok
+            readers[k] = []
+        for b in bank:
+            banks.setdefault(b, {})[q] = tok
+
+    def load(eng, name, s, out, in_):
+        eng.dma_start(out, in_).then_inc(sem[s], 16)
+        wrote[name] = (s, 16)
+
+    def push(src_name, sname, R, back=0):
+        wait("g", [wrote[k] for k in R])
+        sent[0] += send(way[MSG[sname][3]], src_name, sname, back)
+
+    def landed(name, sname):
+        wrote[name] = (sname, arrives[MSG[sname][3]])
+
+    AO, AF = AluOpType, ActivationFunctionType
+    v, te, sc = g.vector, g.tensor, g.scalar
+
+    def ts(out, in0, s1, o0, s2=None, o1=None):
+        if o1 is None:
+            return lambda: v.tensor_scalar(out, in0, s1, None, o0)
+        return lambda: v.tensor_scalar(out, in0, s1, s2, o0, o1)
+
+    def tt(out, a, b, o):
+        return lambda: v.tensor_tensor(out, a, b, o)
+
+    def tc(out, in_):
+        return lambda: v.tensor_copy(out, in_)
+
+    def mm(out, lhsT, rhs, start=True, stop=True):
+        return lambda: te.matmul(out, lhsT, rhs, start, stop)
+
+    def scan(out, mask, data):
+        return lambda: v.tensor_tensor_scan(out, mask, data, 0.0, AO.mult, AO.max)
+
+    def act(out, in_):
+        return lambda: sc.activation(out, in_, AF.Copy)
+
+    n0 = 8 * SIZES[0]
+    load(g.scalar, "cus", "lcu", T.cus[:], T.cu[:])
+    load(g.sync, ("C", 0), "lck0", T.C[:, DUMP:DUMP + n0], T.ck[:, 0:n0])
+    load(g.sync, "L", "lla", T.L[:], T.la[:])
+    load(g.sync, "gaps", "lgap", T.gaps[:], T.gap[:])
+    load(g.sync, ("C", 1), "lck1", T.C[:, DUMP + n0:DUMP + W], T.ck[:, n0:W])
+
+    op("g", [], ["i5"], lambda: g.iota(T.i5[:], [[0, 12]], 0, 8))
+    op("g", [], ["i6"], lambda: g.iota(T.i6[:], [[128, 12]], 0, 0))
+    op("g", [], ["i2"], lambda: g.iota(T.i2[:], [[1, 128]], 0, -1))
+    op("g", [], ["i1"], lambda: g.iota(T.i1[:], [[1, 512]], 0, -16))
+    op("g", [], ["i3"], lambda: g.iota(T.i3[:], [[16, 8], [0, 16]], 15, -1))
+    op("g", [], ["i4"], lambda: g.iota(T.i4[:], [[1, M]], 0, -1))
+
+    op("v", ["i5"], ["i5"], ts(T.i5[:], T.i5[:], 127, AO.bitwise_and))
+    op("v", [], ["RM"], lambda: v.memset(T.RM[:], 1.0))
+    op("v", ["i5", "i6"], ["b8"], tt(T.b8[:], T.i5[:], T.i6[:], AO.add))
+    op("v", [], ["RM"], lambda: v.memset(T.RM[:, 0:16 * NM:16], 0.0))
+    op("v", ["b8", "cus"], ["I0f"], tt(T.I0f[:], T.b8[:], T.cus[:], AO.add))
+    op("v", ["I0f"], ["I0u"], tc(T.I0u[:], T.I0f[:]))
+    op("v", ["cus"], ["cuf"], tc(T.cuf[:], T.cus[:]))
+    op("v", ["i2"], ["ID"], ts(T.ID[:], T.i2[:], 0.0, AO.is_equal))
+    op("v", ["i2"], ["NI"], ts(T.NI[:], T.i2[:], 0.0, AO.is_equal, -BIG, AO.mult))
+    op("v", ["i1"], ["i1"], ts(T.i1[:], T.i1[:], 511, AO.bitwise_and))
+    op("v", ["i3"], ["i3"], ts(T.i3[:], T.i3[:], 4, AO.arith_shift_right))
+    op("v", ["i4"], ["i4"], ts(T.i4[:], T.i4[:], 15, AO.bitwise_and))
+    op("v", ["i1"], ["EX"], ts(T.EX[:], T.i1[:], 16.0, AO.is_lt, BIG, AO.mult))
+    op("v", ["i2"], ["N4"], ts(T.N4[:], T.i2[:], 0.0, AO.is_equal, -4.0, AO.mult))
+    op("v", ["i3"], ["BP"], ts(T.BP[:], T.i3[:], 0.0, AO.is_equal, CB, AO.mult))
+    op("v", ["i3"], ["BN"], ts(T.BN[:], T.i3[:], 0.0, AO.is_equal, -CB, AO.mult))
+    op("v", ["i2"], ["HB0"], ts(T.HB[:, 0:NM], T.i2[:, 0:NM], 0.0, AO.mult, HALF, AO.add))
+    op("v", ["i2"], ["HB1"], ts(T.HB[:, NM:2 * NM], T.i2[:, 0:NM], 0.0, AO.mult, -HALF, AO.add))
+    op("v", ["i4"], ["DM"], ts(T.DM[:], T.i4[:], 0.0, AO.is_gt, 1.0e6, AO.mult))
+    for k in range(K):
+        q, c = SIZES[k] // 16, OFF[k] // 16
+        o = GO[k] + SIZES[k]
+        op("v", ["b8"], [("b5", k)], ts(T.GB[:, o:o + q], T.b8[:, c:c + q], -3.0, AO.add))
+        op("v", ["b8"], [("b188", k)], ts(T.GB[:, o + q:o + 2 * q], T.b8[:, c:c + q], float(DUMP - 4), AO.add))
+    op("v", ["b8"], ["cd"], ts(T.cd[:], T.b8[:], 0.125, AO.mult))
+
+    allC = [("C", 0), ("C", 1)]
+
+    def cl(s, k):
+        return s * 12 + OFF[k] // 16, s * 12 + (OFF[k] + SIZES[k]) // 16
+
+    def sl(name, s, k):
+        return T[name][:, s * M + OFF[k]:s * M + OFF[k] + SIZES[k]]
+
+    def big(name, s, k, a=0, b=None):
+        o = s * E + 16 * OFF[k]
+        return T[name][:, o + 16 * a:o + 16 * (SIZES[k] if b is None else b)]
+
+    def lasts(name, s, k):
+        o = s * E + 16 * OFF[k]
+        return T[name][:, o + 15:o + 16 * SIZES[k]:16]
+
+    def xb(k, m, a, b):
+        o = 16 * OFF[k] + 512 * m
+        return T.xp[:, o + a:o + b]
+
+    def ideal(s, k):
+        n = SIZES[k]
+        if s == 0:
+            return T.Io0[:, OFF[k]:OFF[k] + n], ("Io", k)
+        o = s * MT + MO[k]
+        return T.Ms[:, o:o + n], ("M", s, k)
+
+    def base(s, k):
+        n = SIZES[k]
+        if s == 0:
+            return ideal(0, k)
+        o = s * MT + MO[k] + n
+        return T.Ms[:, o:o + n], ("M", s, k)
+
+    def place(s, k):
+        n = SIZES[k]
+        if s == 0:
+            return T.cuf[:, OFF[k] // 16:(OFF[k] + n) // 16], "cuf"
+        o = s * MT + MO[k] + 2 * n
+        return T.Ms[:, o:o + n // 16], ("M", s, k)
+
+    def gather(q, R, Wk, out, win, off):
+        if q == "v":
+            op("v", R, Wk, tc(out, win.indirect(off)))
+        else:
+            op("a", R, Wk, act(out, win.indirect(off)))
+
+    def first(k):
+        o, n = OFF[k], SIZES[k]
+        keys = [("C", 0)] if k == 0 else allC
+        gather("a", ["I0u"] + keys, [("Io", k)], T.Io0[:, o:o + n], T.C[:, DUMP:DUMP + 8 * (o + n)],
+               T.I0u[:, o // 16:(o + n) // 16])
+        op("v", [("Io", k)], [("J", 0, k)], tc(T.J0[:, o:o + n], T.Io0[:, o:o + n]))
+
+    def stL(s, k):
+        n = SIZES[k]
+        if s == 0:
+            J, j0 = T.J0, OFF[k]
+        else:
+            landed(("J", s, k), "aJ%d_%d" % (s, k))
+            J, j0 = T.J, s * M + OFF[k]
+        nv = (VL0 if s == 0 else VL)[k]
+        na = n - nv
+        if na:
+            gather("a", [("J", s, k), "L"], [("A", s, k, 0)], big("A", s, k, 0, na), T.L[:], J[:, j0:j0 + na])
+        if nv:
+            gather("v", [("J", s, k), "L"], [("A", s, k, 1)], big("A", s, k, na, n), T.L[:], J[:, j0 + na:j0 + n])
+
+    def akeys(s, k):
+        return [("A", s, k, 0), ("A", s, k, 1)]
+
+    def stP(s, k):
+        n = SIZES[k]
+        op("v", akeys(s, k) + ["RM"], [("P", s, k)], scan(big("P", s, k), T.RM[:, 0:16 * n], big("A", s, k)))
+        for m in range(n // 32):
+            op("p", akeys(s, k) + ["NI"], [("X", s, k, m)],
+               mm(xb(k, m, 0, 512), T.NI[:], big("A", s, k, 32 * m, 32 * m + 32), True, False), [(k, m)])
+        op("p", [("P", s, k), "ID"], [("tp", s, k)], mm(T.tp[0:n, 0:128], lasts("P", s, k), T.ID[:]), ["tp"])
+        o = 128 * (s * K + k)
+        op("a", [("tp", s, k)], [("tT", s, k)], act(T.tT[0:n, o:o + 128], T.tp[0:n, 0:128]), ["tp"])
+        for m in range(n // 32):
+            op("p", [("tT", s, k), "EX"], [("X", s, k, m)],
+               mm(xb(k, m, 0, 512), T.tT[32 * m:32 * m + 32, o:o + 128], T.EX[32 * m:32 * m + 32, :], False, True),
+               [(k, m)])
+
+    def stV(s, k, m):
+        op("v", akeys(s, k) + [("X", s, k, m)], [("V", s, k, m)],
+           tt(big("V", s, k, 32 * m, 32 * m + 32), xb(k, m, 0, 512), big("A", s, k, 32 * m, 32 * m + 32), AO.min),
+           [(k, m)])
+
+    def stS(s, k):
+        n = SIZES[k]
+        op("v", [("V", s, k, m) for m in range(n // 32)] + ["RM"], [("S", s, k)],
+           scan(big("S", s, k), T.RM[:, 0:16 * n], big("V", s, k)))
+        op("v", [("S", s, k)], [("su", s, k)], tc(sl("su", s, k), lasts("S", s, k)))
+
+    def stN(s, k):
+        n = SIZES[k]
+        q = n // 16
+        c0, c1 = cl(s, k)
+        if s > 0:
+            landed(("M", s, k), "aM%d_%d" % (s, k))
+        y, yk = place(s, k)
+        o = 24 * s + OFF[k] // 8
+        op("a", [yk], [("sg", s, k)], lambda: sc.activation(T.sg[:, o:o + q], y, AF.Sign, bias=-6.5))
+        op("a", [yk], [("sh", s, k)], lambda: sc.activation(T.sg[:, o + q:o + 2 * q], y, AF.Sign, bias=-7.5))
+        b = [(k, 1)]
+        p0 = 2 * n
+        N = ("N", s, k)
+        if s == 0:
+            I, ik = ideal(s, k)
+            gk = ("gb", k)
+            op("p", [ik, "ID"], [N], mm(xb(k, 1, 0, n), T.ID[:], I, True, False), b)
+            op("p", [ik, "ID"], [N], mm(xb(k, 1, n, p0), T.ID[:], I, False, False), b)
+            op("p", [yk, "ID"], [N], mm(xb(k, 1, p0, p0 + q), T.ID[:], y, False, False), b)
+        else:
+            m = s * MT + MO[k]
+            gk = "GB%d" % s
+            if gk not in wrote:
+                landed(gk, "agap%d" % s)
+            op("p", [yk, "ID"], [N], mm(xb(k, 1, 0, p0 + q), T.ID[:], T.Ms[:, m:m + p0 + q], True, False), b)
+        op("p", [yk, "ID"], [N], mm(xb(k, 1, p0 + q, p0 + 2 * q), T.ID[:], y, False, False), b)
+        gs = s * GW + GO[k]
+        op("p", [gk, ("b5", k), ("b188", k)], [N],
+           mm(xb(k, 1, n, p0 + 2 * q), T.ID[:], T.GB[:, gs:gs + n + 2 * q], False, False), b)
+        op("p", [("sg", s, k), ("sh", s, k), "N4"], [N],
+           mm(xb(k, 1, p0, p0 + 2 * q), T.N4[:], T.sg[:, o:o + 2 * q], False, True), b)
+        op("v", [N], [("Ru", s, k)], tc(T.Ru[:, c0:c1], xb(k, 1, p0, p0 + q)), b)
+
+    def stG(s, k):
+        n = SIZES[k]
+        nv = VG[k]
+        na = n - nv
+        win = T.C[:, DUMP:DUMP + W]
+        o = s * M + OFF[k]
+        if na:
+            gather("a", [("su", s, k)] + allC, [("B", s, k, 0)], big("BB", s, k, 0, na), win, T.su[:, o:o + na])
+        if nv:
+            gather("v", [("su", s, k)] + allC, [("B", s, k, 1)], big("BB", s, k, na, n), win, T.su[:, o + na:o + n])
+
+    def stR(s, k):
+        c0, c1 = cl(s, k)
+        gather("a", [("Ru", s, k)] + allC, [("RR", s, k)], sl("RR", s, k), T.C[:, DUMP:DUMP + W], T.Ru[:, c0:c1])
+
+    def stZ(s, k):
+        n = SIZES[k]
+        In, GE = sl("In", s, k), sl("GE", s, k)
+        op("v", [("B", s, k, 0), ("B", s, k, 1), "RM"], [("Z", s, k)],
+           scan(big("Z", s, k), T.RM[:, 0:16 * n], big("BB", s, k)))
+        op("v", [("Z", s, k), ("N", s, k)], [("In", s, k)], tt(In, xb(k, 1, 0, n), lasts("Z", s, k), AO.max), [(k, 1)])
+        op("v", [("In", s, k), ("N", s, k)], [("GE", s, k)], tt(GE, In, xb(k, 1, n, 2 * n), AO.is_ge), [(k, 1)])
+        b = [(k, 0)]
+        op("p", ["BP", "HB0", "HB1"], [("+", s, k)],
+           mm(xb(k, 0, 0, 2 * n), T.BP[:], T.HB[:, NM - n:NM + n], True, False), b)
+        op("p", [("GE", s, k)], [("+", s, k)], mm(xb(k, 0, 0, n), T.BP[:], GE, False, False), b)
+        op("p", [("GE", s, k), "BN"], [("+", s, k)], mm(xb(k, 0, n, 2 * n), T.BN[:], GE, False, True), b)
+
+    def stF(s, k):
+        n = SIZES[k]
+        if s < ST - 1:
+            o = (s + 1) * MT + MO[k]
+            out, key = T.oMs[:, o:o + n], ("oI", s + 1, k)
+        else:
+            out, key = T.oF[:, OFF[k]:OFF[k] + n], ("oF", k)
+        b = [(k, 0)]
+        m1, m2 = sl("m1", s, k), xb(k, 0, 2 * n, 3 * n)
+        op("v", [("+", s, k), ("RR", s, k)], [("m1", s, k)], tt(m1, xb(k, 0, 0, n), sl("RR", s, k), AO.min), b)
+        op("v", [("+", s, k), ("In", s, k)], [("m2", s, k)], tt(m2, xb(k, 0, n, 2 * n), sl("In", s, k), AO.min), b)
+        op("v", [("m1", s, k), ("m2", s, k)], [key], tt(out, m2, m1, AO.max), b)
+        if s < ST - 1:
+            op("v", [key], [("oJ", s + 1, k)], tc(sl("oJ", s + 1, k), out))
+            push("oJ", "aJ%d_%d" % (s + 1, k), [("oJ", s + 1, k)])
+        else:
+            push("oF", "aF%d" % k, [key])
+
+    def stX(s, k):
+        n = SIZES[k]
+        q = n // 16
+        c = OFF[k] // 16
+        D, DS = sl("DD", s, k), sl("DS", s, k)
+        b0 = [(k, 0)]
+        op("v", [("+", s, k), "DM"], [("DD", s, k)], tt(D, xb(k, 0, 0, n), T.DM[:, OFF[k]:OFF[k] + n], AO.is_ge), b0)
+        if s < ST - 1:
+            o = (s + 1) * MT + MO[k]
+            m2 = xb(k, 0, 3 * n, 4 * n)
+            t, tk = base(s, k)
+            op("v", [("+", s, k), tk], [("m3", s, k)], tt(m2, xb(k, 0, n, 2 * n), t, AO.min), b0)
+        op("v", [("DD", s, k), "RM"], [("DS", s, k)], scan(DS, T.RM[:, 0:n], D))
+        if s < ST - 1:
+            op("v", [("m3", s, k), ("m1", s, k)], [("oT", s + 1, k)],
+               tt(T.oMs[:, o + n:o + 2 * n], m2, sl("m1", s, k), AO.max), b0)
+        y, yk = place(s, k)
+        os = s * M + OFF[k]
+        ls = T.DS[:, os + 15:os + n:16]
+        if s < ST - 1:
+            op("v", [("DS", s, k), yk], [("oy", s + 1, k)], tt(T.oMs[:, o + 2 * n:o + 2 * n + q], y, ls, AO.add))
+            push("oMs", "aM%d_%d" % (s + 1, k), [("oI", s + 1, k), ("oT", s + 1, k), ("oy", s + 1, k)])
+            op("v", [("DS", s, k), ("N", s, k)], [("wo", s, k)],
+               tt(T.wo[:, 12 * s + c:12 * s + c + q], xb(k, 1, 2 * n + q, 2 * n + 2 * q), ls, AO.mult), [(k, 1)])
+        else:
+            op("v", [("DS", s, k), yk], [("y", k)], tt(T.Ry[:, c:c + q], y, ls, AO.add))
+
+    def tail(s):
+        ks = range(K)
+        wo, ou = T.wo[:, 12 * s:12 * s + 12], T.ou[:, 12 * s:12 * s + 12]
+        op("v", [("wo", s, k) for k in ks] + ["cd"], [("wo", s)], tt(wo, wo, T.cd[:], AO.max))
+        op("v", [("wo", s)], [("ou", s)], tc(ou, wo))
+        op("v", [("ou", s)] + [("In", s, k) for k in ks], allC,
+           tc(T.C[:, 0:DUMP + W].indirect(ou), T.In[:, s * M:s * M + M]))
+
+    stages = {"L": stL, "P": stP, "V": stV, "S": stS, "N": stN, "G": stG, "R": stR, "Z": stZ, "F": stF, "X": stX,
+              "T": tail}
+
+    for k in range(K):
+        first(k)
+        if k == 0:
+            stL(0, 0)
+            for kk in range(K):
+                op("v", ["gaps"], [("gb", kk)],
+                   tc(T.GB[:, GO[kk]:GO[kk] + SIZES[kk]], T.gaps[:, OFF[kk]:OFF[kk] + SIZES[kk]]))
+    push("GB", "agap1", [(x, k) for x in ("gb", "b5", "b188") for k in range(K)], GW)
+    landed("GB1", "agap1")
+    push("GB", "agap2", ["GB1"], GW)
+    for t in ORDER:
+        if t != "0L0":
+            stages[t[1]](int(t[0]), *[int(x) for x in t[2:]])
+    yk = [("y", k) for k in range(K)]
+    op("v", yk, ["oFq"], ts(T.oFq[:], T.Ry[:], 8.0, AO.is_ge, -8.0, AO.mult))
+    op("v", yk + ["oFq"], ["oFy"], tt(T.oFy[:], T.Ry[:], T.oFq[:], AO.add))
+    push("oFy", "aFy", ["oFy"])
+
+    total = 0
+    for k in range(K):
+        landed(("F", k), "aF%d" % k)
+        wait("s", [wrote[("F", k)]])
+        g.sync.dma_start(T.yi[:, OFF[k]:OFF[k] + SIZES[k]], T.F[:, OFF[k]:OFF[k] + SIZES[k]]).then_inc(sem.st, 16)
+        total += 16
+    landed("Fy", "aFy")
+    wait("s", [wrote["Fy"]])
+    g.sync.dma_start(T.yc[:], T.Fy[:]).then_inc(sem.st, 16)
+    total += 16
+    g.sync.wait_ge(sem.st, total)
+    g.wait_ge(sem.ls, sent[0])
+    for q, s in (("v", "v"), ("a", "a"), ("p", "p"), ("g", "gq")):
+        g.wait_ge(sem[s], count[q])

@@ -1,99 +1,128 @@
 from concourse.mybir import AluOpType, ActivationFunctionType
 
 M, B, H, ST, W = 192, 8, 5, 3, 1536
-SIZES = [96, 96]
+SIZES = [64, 64, 64]
 K = len(SIZES)
 OFF = [sum(SIZES[:k]) for k in range(K)]
+NM = max(SIZES)
+Q = M // 16
+QS = 2 * -(-NM // 32)
 DUMP = M
 BIG = 2048.0
-CB = 4096.0
-HALF = -(H - 0.5) / 16.0
-VL0 = [48, 0]
-VL = [48, 0]
-VG = [0, 0]
-ORDER = """
-0L0 0P0 0V01 0V02 0V00 0S0 0N0 0L1 0P1 0V10 0V11 0G0 0R0 0V12 0Z0 0S1 0F0 0X0 0N1 0G1 0R1 0Z1 0F1 1L0 1P0 0X1 0T
-1V01 1V00 1V02 1N0 1L1 1P1 1S0 1V10 1V11 1V12 1S1 1N1 1G0 1R0 1G1 1R1 1Z0 1F0 1X0 1Z1 1F1 1X1 2L0 2P0 1T
-2V01 2V02 2V00 2N0 2L1 2R0 2P1 2S0 2V10 2G0 2V11 2V12 2S1 2N1 2G1 2Z0 2F0 2R1 2Z1 2X0 2F1 2X1
-""".split()
+CB = 2 * BIG
+LAST = ST * K - 1
+SHARE = {("L", 1): 32, ("G", 17): 32}
+RELOAD_ON = "a"
+TURN_ON = None
+PIECE = 32
+HALVES = 1
+XB = 3
 
-E = 16 * M
-MW = [2 * n + n // 16 for n in SIZES]
-MO = [sum(MW[:k]) for k in range(K)]
-MT = sum(MW)
-GO = [OFF[k] + OFF[k] // 8 for k in range(K)]
-GW = M + M // 8
-NM = max(SIZES)
+_R = ("P1.0 n1.0 S0.1 U0.1 J2 L1.1 N0 G0.0 G0.1 H-1 P1.1 x1.0 Z0.0 n1.1 A1.0 Z0.1 I0 x1.1 C1 R0 S1.0 t0 L2.0 D1 E0 U1.0 "
+      "A1.1 F0 Y0 T0")
+ROUND = {False: _R, True: _R}
+
+
+def order(stages):
+    out = []
+    for t in range(-4, LAST + 4):
+        for x in stages.split():
+            i, _, a = x[1:].partition(".")
+            i = t + int(i)
+            if 0 <= i <= LAST:
+                out.append(x[0] + str(i) + ("." + (a or "0") if x[0] in "LPSUGZABnoxw" else ""))
+    return out + ["O"]
+
+
+ORDERS = {r: order(ROUND[r]) for r in ROUND}
+
+
+def pad8(x):
+    return -(-x // 8) * 8
+
+
+GO = [sum(pad8(n + n // 16) for n in SIZES[:k]) for k in range(K + 1)]
+GY = GO[K]
+GW = GY + 2 * Q
+HO = [sum(pad8(4 * n + n // 8) for n in SIZES[:k]) for k in range(K + 1)]
 SCRATCH = {
     "C": ("sbuf", [128, DUMP + W], "int32"),
     "L": ("sbuf", [128, W], "int32"),
-    "cus": ("sbuf", [128, 12], "int32"),
+    "cus": ("sbuf", [128, Q], "int32"),
     "gaps": ("sbuf", [128, M], "int32"),
     "GB": ("sbuf", [128, ST * GW], "float16"),
     "RM": ("sbuf", [128, 16 * NM], "bfloat16"),
-    "EX": ("sbuf", [128, 512], "float16"),
-    "ID": ("sbuf", [128, 128], "float16"),
-    "N4": ("sbuf", [128, 128], "float16"),
-    "NI": ("sbuf", [128, 128], "float16"),
-    "BP": ("sbuf", [128, 128], "float16"),
-    "BN": ("sbuf", [128, 128], "float16"),
     "HB": ("sbuf", [128, 2 * NM], "float16"),
-    "DM": ("sbuf", [128, M], "float32"),
-    "i1": ("sbuf", [128, 512], "int32"),
+    "MK": ("sbuf", [128, NM], "float16"),
+    "EX": ("sbuf", [128, 8 * NM], "float16"),
+    "tT": ("sbuf", [128, ST * K * 128], "float16"),
+    "i1": ("sbuf", [128, 8 * NM], "int32"),
     "i2": ("sbuf", [128, 128], "int32"),
     "i3": ("sbuf", [128, 128], "int32"),
-    "i4": ("sbuf", [128, M], "int32"),
-    "i5": ("sbuf", [128, 12], "int32"),
-    "i6": ("sbuf", [128, 12], "int32"),
-    "b8": ("sbuf", [128, 12], "float32"),
-    "cd": ("sbuf", [128, 12], "float32"),
-    "I0f": ("sbuf", [128, 12], "float32"),
-    "I0u": ("sbuf", [128, 12], "uint16"),
-    "cuf": ("sbuf", [128, 12], "float16"),
-    "Io0": ("sbuf", [128, M], "float16"),
-    "J0": ("sbuf", [128, M], "uint16"),
-    "wo": ("sbuf", [128, 12 * ST], "float32"),
-    "ou": ("sbuf", [128, 12 * ST], "uint16"),
-    "sg": ("sbuf", [128, 24 * ST], "float16"),
-    "Ru": ("sbuf", [128, 12 * ST], "uint16"),
-    "Ry": ("sbuf", [128, 12], "float32"),
-    "Fy": ("sbuf", [128, 12], "float32"),
-    "oFy": ("sbuf", [128, 12], "float32"),
-    "oFq": ("sbuf", [128, 12], "float32"),
+    "i4": ("sbuf", [128, NM], "int32"),
+    "I0": ("sbuf", [128, M], "float16"),
+    "Ru": ("sbuf", [128, ST * K * QS], "uint16"),
+    "sg": ("sbuf", [128, ST * Q], "float16"),
+    "sh": ("sbuf", [128, Q], "float16"),
+    "ou": ("sbuf", [128, ST * Q], "uint16"),
+    "I0u": ("sbuf", [128, K * QS], "uint16"),
     "J": ("sbuf", [128, ST * M], "uint16"),
     "oJ": ("sbuf", [128, ST * M], "uint16"),
-    "Ms": ("sbuf", [128, ST * MT], "float16"),
-    "oMs": ("sbuf", [128, ST * MT], "float16"),
-    "F": ("sbuf", [128, M], "float32"),
-    "oF": ("sbuf", [128, M], "float32"),
-    "tT": ("sbuf", [128, ST * K * 128], "float16"),
-    "xp": ("psum", [128, E], "float32"),
-    "tp": ("psum", [128, 512], "float32"),
+    "oH": ("sbuf", [128, HO[K]], "float16"),
+    "H1": ("sbuf", [128, HO[K]], "float16"),
+    "H2": ("sbuf", [128, HO[K]], "float16"),
+    "oF": ("sbuf", [128, M + Q], "float32"),
+    "px": ("psum", [128, 3 * 512], "float32"),
+    "pn": ("psum", [128, 2 * 512], "float32"),
+    "py": ("psum", [128, 512], "float32"),
+    "pm": ("psum", [128, 512], "float32"),
+    "pa": ("psum", [128, 512], "float32"),
 }
-for _n in ("A", "P", "V", "S", "BB", "Z"):
-    SCRATCH[_n] = ("sbuf", [128, ST * E], "float16")
-for _n, _d in (("su", "uint16"), ("RR", "float16"), ("In", "float16"), ("GE", "float16"),
-               ("m1", "float16"), ("DD", "float16"), ("DS", "float16")):
+for _k in range(K):
+    SCRATCH["F%d" % _k] = ("dram", [128, SIZES[_k] + Q * (_k == K - 1)], "float32")
+for _n in ("ID", "NG", "NI", "PI", "N4", "BP", "BN"):
+    SCRATCH[_n] = ("sbuf", [128, 128], "float16")
+for _n in ("i5", "i6", "i7"):
+    SCRATCH[_n] = ("sbuf", [128, Q], "int32")
+for _n in ("b8", "cd", "I0f", "R0f", "W0", "wo0", "wo1", "y1", "y2", "y3"):
+    SCRATCH[_n] = ("sbuf", [128, Q], "float32")
+for _n in ("A", "V", "P", "S", "BB", "Z"):
+    SCRATCH[_n] = ("sbuf", [128, ST * M * 16], "float16")
+for _n, _d in (("su", "uint16"), ("RR", "float16"), ("In", "float16"), ("GE", "float16"), ("m2", "float16"),
+               ("DS", "float16")):
     SCRATCH[_n] = ("sbuf", [128, ST * M], _d)
-SEMAPHORES = ["v", "a", "p", "gq", "ls", "lcu", "lck0", "lck1", "lla", "lgap", "agap1", "agap2", "aFy", "st"]
-for _k in range(K):
-    for _s in range(1, ST):
-        SEMAPHORES += ["aJ%d_%d" % (_s, _k), "aM%d_%d" % (_s, _k)]
-    SEMAPHORES += ["aF%d" % _k]
+SEMAPHORES = ["v", "a", "p", "gq", "ls", "lcu", "lla", "lgap", "st", "aG1_0", "aG1_1", "aG2"]
+SEMAPHORES += ["lck%d" % _k for _k in range(K)]
+SEMAPHORES += ["a%s%d" % (_n, _i) for _n in "JH" for _i in range(K, ST * K)] + ["aF%d" % _k for _k in range(K)]
 
-MSG = {"agap1": ("GB", GW, 2 * GW, 1), "agap2": ("GB", 2 * GW, 3 * GW, 1), "aFy": ("Fy", 0, 12, 1)}
+GH = pad8(GW // 2)
+MSG = {"aG1_0": ("GB", GW, GH, "GB", 0, 0), "aG1_1": ("GB", GW + GH, GW - GH, "GB", GH, 1),
+       "aG2": ("GB", 2 * GW, GW, "GB", GW, 1)}
+GAPS = [["gg"], ["aG1_0", "aG1_1"], ["aG2"]]
 for _k in range(K):
-    for _s in range(1, ST):
-        MSG["aJ%d_%d" % (_s, _k)] = ("J", _s * M + OFF[_k], _s * M + OFF[_k] + SIZES[_k], 0)
-        MSG["aM%d_%d" % (_s, _k)] = ("Ms", _s * MT + MO[_k], _s * MT + MO[_k] + MW[_k], 1)
-    MSG["aF%d" % _k] = ("F", OFF[_k], OFF[_k] + SIZES[_k], 0)
-ISSUE = ["agap1", "agap2"]
-for _t in ORDER:
-    if _t[1] == "F":
-        ISSUE.append("aJ%d_%s" % (int(_t[0]) + 1, _t[2]) if int(_t[0]) < ST - 1 else "aF" + _t[2])
-    if _t[1] == "X" and int(_t[0]) < ST - 1:
-        ISSUE.append("aM%d_%s" % (int(_t[0]) + 1, _t[2]))
-ISSUE.append("aFy")
+    _n, _q = SIZES[_k], SIZES[_k] // 16
+    for _s in (1, 2):
+        MSG["aJ%d" % (_s * K + _k)] = ("J", _s * M + OFF[_k], _n, "oJ", _s * M + OFF[_k], 0)
+    MSG["aH%d" % (K + _k)] = ("H1", HO[_k], 2 * _n + _q, "oH", HO[_k], 1)
+    MSG["aH%d" % (2 * K + _k)] = ("H2", HO[_k], 2 * _n + 2 * _q, "H1", HO[_k] + 2 * _n, 1)
+    MSG["aF%d" % _k] = ("F%d" % _k, 0, _n + Q * (_k == K - 1), "oF", OFF[_k], 0)
+
+
+def issue(tokens):
+    out = []
+    for t in tokens:
+        i = int(t[1:]) if t[0] in "FH" else None
+        if t == "C0":
+            out += ["aG1_0", "aG1_1"]
+        elif t[0] == "F" and i < LAST:
+            out.append("aJ%d" % (i + K) if i < 2 * K else "aF%d" % (i - 2 * K))
+        elif t[0] == "H" and i < 2 * K:
+            out.append("aH%d" % (i + K))
+            if i == 0:
+                out.append("aG2")
+        elif t == "O":
+            out.append("aF%d" % (K - 1))
+    return out
 
 
 def lanes(topo, cores, src, dst):
@@ -114,11 +143,16 @@ def rank_program(g, core, T, topo):
     sem = T.sem
     rank = T.rank_of(core)
 
-    def send(dst, src_name, sname, back=0):
-        name, c0, c1 = MSG[sname][:3]
+    def tokens(r):
+        return ORDERS[not topo.may_write(cores[(r - 1) % n_ranks], cores[r])]
+
+    def send(dst, sname, relay):
+        name, c, n, src, cs = MSG[sname][:5]
+        if relay:
+            src, cs = name, c
         rid, pid = topo.addr(dst, core)
         m = topo.mask(core, dst)
-        g.remote_dma(T[name][:, c0:c1], T[src_name][:, c0 - back:c1 - back], sem[sname], sem.ls, pid, rid, m)
+        g.remote_dma(T[name][:, c:c + n], T[src][:, cs:cs + n], sem[sname], sem.ls, pid, rid, m)
         return nbits(m)
 
     if rank is None:
@@ -128,11 +162,10 @@ def rank_program(g, core, T, topo):
             way = lanes(topo, cores, src, dst)
             if core not in way:
                 continue
-            for sname in ISSUE:
-                name, c0, c1, lane = MSG[sname]
-                if way[lane] == core:
+            for sname in issue(tokens(r)):
+                if way[MSG[sname][5]] == core:
                     g.wait_ge(sem[sname], nbits(topo.mask(src, core)))
-                    total += send(dst, name, sname)
+                    total += send(dst, sname, True)
         if total:
             g.wait_ge(sem.ls, total)
         return
@@ -157,14 +190,14 @@ def rank_program(g, core, T, topo):
                 queues[q][0].wait_ge(sem[s], need[s])
                 seen[q][s] = need[s]
 
-    def op(q, R, Wk, call, bank=()):
-        d = [wrote[k] for k in R if k in wrote]
+    def op(q, R, Wk, call, bank=None, group=False):
+        d = [wrote[k] for k in R]
         for k in Wk:
-            if k in wrote:
+            if k in wrote and not group:
                 d.append(wrote[k])
             d += readers.get(k, [])
-        for b in bank:
-            d += [t for qq, t in banks.get(b, {}).items() if qq != q]
+        if bank is not None:
+            d += [t for qq, t in banks.get(bank, {}).items() if qq != q]
         wait(q, d)
         s = queues[q][1]
         call().then_inc(sem[s], 1)
@@ -175,19 +208,19 @@ def rank_program(g, core, T, topo):
         for k in Wk:
             wrote[k] = tok
             readers[k] = []
-        for b in bank:
-            banks.setdefault(b, {})[q] = tok
+        if bank is not None:
+            banks.setdefault(bank, {})[q] = tok
 
     def load(eng, name, s, out, in_):
         eng.dma_start(out, in_).then_inc(sem[s], 16)
         wrote[name] = (s, 16)
 
-    def push(src_name, sname, R, back=0):
+    def push(sname, R):
         wait("g", [wrote[k] for k in R])
-        sent[0] += send(way[MSG[sname][3]], src_name, sname, back)
+        sent[0] += send(way[MSG[sname][5]], sname, False)
 
-    def landed(name, sname):
-        wrote[name] = (sname, arrives[MSG[sname][3]])
+    for sname in MSG:
+        wrote[sname] = (sname, arrives[MSG[sname][5]])
 
     AO, AF = AluOpType, ActivationFunctionType
     v, te, sc = g.vector, g.tensor, g.scalar
@@ -203,295 +236,345 @@ def rank_program(g, core, T, topo):
     def tc(out, in_):
         return lambda: v.tensor_copy(out, in_)
 
-    def mm(out, lhsT, rhs, start=True, stop=True):
-        return lambda: te.matmul(out, lhsT, rhs, start, stop)
-
     def scan(out, mask, data):
         return lambda: v.tensor_tensor_scan(out, mask, data, 0.0, AO.mult, AO.max)
 
-    def act(out, in_):
-        return lambda: sc.activation(out, in_, AF.Copy)
+    def act(out, in_, fn, bias=0.0, scale=1.0):
+        return lambda: sc.activation(out, in_, fn, bias=bias, scale=scale)
 
-    n0 = 8 * SIZES[0]
-    load(g.scalar, "cus", "lcu", T.cus[:], T.cu[:])
-    load(g.sync, ("C", 0), "lck0", T.C[:, DUMP:DUMP + n0], T.ck[:, 0:n0])
-    load(g.sync, "L", "lla", T.L[:], T.la[:])
-    load(g.sync, "gaps", "lgap", T.gaps[:], T.gap[:])
-    load(g.sync, ("C", 1), "lck1", T.C[:, DUMP + n0:DUMP + W], T.ck[:, n0:W])
-
-    op("g", [], ["i5"], lambda: g.iota(T.i5[:], [[0, 12]], 0, 8))
-    op("g", [], ["i6"], lambda: g.iota(T.i6[:], [[128, 12]], 0, 0))
-    op("g", [], ["i2"], lambda: g.iota(T.i2[:], [[1, 128]], 0, -1))
-    op("g", [], ["i1"], lambda: g.iota(T.i1[:], [[1, 512]], 0, -16))
-    op("g", [], ["i3"], lambda: g.iota(T.i3[:], [[16, 8], [0, 16]], 15, -1))
-    op("g", [], ["i4"], lambda: g.iota(T.i4[:], [[1, M]], 0, -1))
-
-    op("v", ["i5"], ["i5"], ts(T.i5[:], T.i5[:], 127, AO.bitwise_and))
-    op("v", [], ["RM"], lambda: v.memset(T.RM[:], 1.0))
-    op("v", ["i5", "i6"], ["b8"], tt(T.b8[:], T.i5[:], T.i6[:], AO.add))
-    op("v", [], ["RM"], lambda: v.memset(T.RM[:, 0:16 * NM:16], 0.0))
-    op("v", ["b8", "cus"], ["I0f"], tt(T.I0f[:], T.b8[:], T.cus[:], AO.add))
-    op("v", ["I0f"], ["I0u"], tc(T.I0u[:], T.I0f[:]))
-    op("v", ["cus"], ["cuf"], tc(T.cuf[:], T.cus[:]))
-    op("v", ["i2"], ["ID"], ts(T.ID[:], T.i2[:], 0.0, AO.is_equal))
-    op("v", ["i2"], ["NI"], ts(T.NI[:], T.i2[:], 0.0, AO.is_equal, -BIG, AO.mult))
-    op("v", ["i1"], ["i1"], ts(T.i1[:], T.i1[:], 511, AO.bitwise_and))
-    op("v", ["i3"], ["i3"], ts(T.i3[:], T.i3[:], 4, AO.arith_shift_right))
-    op("v", ["i4"], ["i4"], ts(T.i4[:], T.i4[:], 15, AO.bitwise_and))
-    op("v", ["i1"], ["EX"], ts(T.EX[:], T.i1[:], 16.0, AO.is_lt, BIG, AO.mult))
-    op("v", ["i2"], ["N4"], ts(T.N4[:], T.i2[:], 0.0, AO.is_equal, -4.0, AO.mult))
-    op("v", ["i3"], ["BP"], ts(T.BP[:], T.i3[:], 0.0, AO.is_equal, CB, AO.mult))
-    op("v", ["i3"], ["BN"], ts(T.BN[:], T.i3[:], 0.0, AO.is_equal, -CB, AO.mult))
-    op("v", ["i2"], ["HB0"], ts(T.HB[:, 0:NM], T.i2[:, 0:NM], 0.0, AO.mult, HALF, AO.add))
-    op("v", ["i2"], ["HB1"], ts(T.HB[:, NM:2 * NM], T.i2[:, 0:NM], 0.0, AO.mult, -HALF, AO.add))
-    op("v", ["i4"], ["DM"], ts(T.DM[:], T.i4[:], 0.0, AO.is_gt, 1.0e6, AO.mult))
-    for k in range(K):
-        q, c = SIZES[k] // 16, OFF[k] // 16
-        o = GO[k] + SIZES[k]
-        op("v", ["b8"], [("b5", k)], ts(T.GB[:, o:o + q], T.b8[:, c:c + q], -3.0, AO.add))
-        op("v", ["b8"], [("b188", k)], ts(T.GB[:, o + q:o + 2 * q], T.b8[:, c:c + q], float(DUMP - 4), AO.add))
-    op("v", ["b8"], ["cd"], ts(T.cd[:], T.b8[:], 0.125, AO.mult))
-
-    allC = [("C", 0), ("C", 1)]
-
-    def cl(s, k):
-        return s * 12 + OFF[k] // 16, s * 12 + (OFF[k] + SIZES[k]) // 16
-
-    def sl(name, s, k):
-        return T[name][:, s * M + OFF[k]:s * M + OFF[k] + SIZES[k]]
-
-    def big(name, s, k, a=0, b=None):
-        o = s * E + 16 * OFF[k]
-        return T[name][:, o + 16 * a:o + 16 * (SIZES[k] if b is None else b)]
-
-    def lasts(name, s, k):
-        o = s * E + 16 * OFF[k]
-        return T[name][:, o + 15:o + 16 * SIZES[k]:16]
-
-    def xb(k, m, a, b):
-        o = 16 * OFF[k] + 512 * m
-        return T.xp[:, o + a:o + b]
-
-    def ideal(s, k):
-        n = SIZES[k]
-        if s == 0:
-            return T.Io0[:, OFF[k]:OFF[k] + n], ("Io", k)
-        o = s * MT + MO[k]
-        return T.Ms[:, o:o + n], ("M", s, k)
-
-    def base(s, k):
-        n = SIZES[k]
-        if s == 0:
-            return ideal(0, k)
-        o = s * MT + MO[k] + n
-        return T.Ms[:, o:o + n], ("M", s, k)
-
-    def place(s, k):
-        n = SIZES[k]
-        if s == 0:
-            return T.cuf[:, OFF[k] // 16:(OFF[k] + n) // 16], "cuf"
-        o = s * MT + MO[k] + 2 * n
-        return T.Ms[:, o:o + n // 16], ("M", s, k)
+    def sums(key, bank, terms, start=True, stop=True):
+        for j, (out, wt, rhs, R) in enumerate(terms):
+            first, last = start and j == 0, stop and j == len(terms) - 1
+            op("p", R + [wt], [key], lambda: te.matmul(out, T[wt][:], rhs, first, last), bank, not first)
 
     def gather(q, R, Wk, out, win, off):
-        if q == "v":
-            op("v", R, Wk, tc(out, win.indirect(off)))
-        else:
-            op("a", R, Wk, act(out, win.indirect(off)))
+        op(q, R, Wk, tc(out, win.indirect(off)) if q == "v" else lambda: sc.activation(out, win.indirect(off), AF.Copy))
+
+    load(g.scalar, "cus", "lcu", T.cus[:], T.cu[:])
+    for k in range(K):
+        a, b = 8 * OFF[k], 8 * (OFF[k] + SIZES[k])
+        load(g.sync, ("C", k), "lck%d" % k, T.C[:, DUMP + a:DUMP + b], T.ck[:, a:b])
+        if k == 0:
+            load(g.sync, "L", "lla", T.L[:], T.la[:])
+    load(g.sync, "gaps", "lgap", T.gaps[:], T.gap[:])
+    allC = [("C", k) for k in range(K)]
+
+    op("g", [], ["i5"], lambda: g.iota(T.i5[:], [[0, Q]], 0, 8))
+    op("g", [], ["i6"], lambda: g.iota(T.i6[:], [[128, Q]], 0, 0))
+    op("g", [], ["i2"], lambda: g.iota(T.i2[:], [[1, 128]], 0, -1))
+    if TURN_ON:
+        op("g", [], ["i1"], lambda: g.iota(T.i1[:], [[1, 8 * NM]], 0, -8))
+    op("g", [], ["i3"], lambda: g.iota(T.i3[:], [[16, 8], [0, 16]], 15, -1))
+    op("g", [], ["i4"], lambda: g.iota(T.i4[:], [[1, NM]], 0, -1))
+
+    op("v", [], ["RM"], lambda: v.memset(T.RM[:], 1.0))
+    op("v", ["i5"], ["i5"], ts(T.i5[:], T.i5[:], 127, AO.bitwise_and))
+    op("v", [], ["RM"], lambda: v.memset(T.RM[:, 0:16 * NM:16], 0.0))
+    op("v", ["i5", "i6"], ["b8"], tt(T.b8[:], T.i5[:], T.i6[:], AO.add))
+    for name, wt in (("ID", 1.0), ("NI", -BIG), ("PI", BIG), ("NG", -1.0), ("N4", -4.0)):
+        op("v", ["i2"], [name], ts(T[name][:], T.i2[:], 0.0, AO.is_equal, wt, AO.mult))
+    op("v", ["b8", "cus"], ["I0f"], tt(T.I0f[:], T.b8[:], T.cus[:], AO.add))
+    op("v", ["cus"], ["i7"], ts(T.i7[:], T.cus[:], 1.0, AO.add))
+    for k in range(K):
+        c, q = OFF[k] // 16, SIZES[k] // 16
+        op("v", ["I0f"], [("I0u", k)], tc(T.I0u[:, QS * k:QS * k + q], T.I0f[:, c:c + q]))
 
     def first(k):
         o, n = OFF[k], SIZES[k]
-        keys = [("C", 0)] if k == 0 else allC
-        gather("a", ["I0u"] + keys, [("Io", k)], T.Io0[:, o:o + n], T.C[:, DUMP:DUMP + 8 * (o + n)],
-               T.I0u[:, o // 16:(o + n) // 16])
-        op("v", [("Io", k)], [("J", 0, k)], tc(T.J0[:, o:o + n], T.Io0[:, o:o + n]))
+        win, off = T.C[:, DUMP:DUMP + 8 * (o + n)], T.I0u[:, QS * k:QS * k + n // 16]
+        gather("v", [("I0u", k)] + allC[:k + 1], [("J", k)], T.J[:, o:o + n], win, off)
+        gather("a", [("I0u", k)] + allC[:k + 1], [("I0", k)], T.I0[:, o:o + n], win, off)
 
-    def stL(s, k):
-        n = SIZES[k]
+    op("v", ["i7"], ["i7"], ts(T.i7[:], T.i7[:], B - 1, AO.bitwise_and))
+    op("v", ["i3"], ["i3"], ts(T.i3[:], T.i3[:], 4, AO.arith_shift_right))
+    first(0)
+    if TURN_ON:
+        op("v", ["i1"], ["i1"], ts(T.i1[:], T.i1[:], 2047, AO.bitwise_and))
+        op("v", ["i1"], ["EX"], ts(T.EX[:], T.i1[:], 8.0, AO.is_lt, BIG, AO.mult))
+    op("v", ["i4"], ["i4"], ts(T.i4[:], T.i4[:], 15, AO.bitwise_and))
+    op("v", ["b8", "i7"], ["R0f"], tt(T.R0f[:], T.b8[:], T.i7[:], AO.add))
+    op("v", ["i3"], ["BP"], ts(T.BP[:], T.i3[:], 0.0, AO.is_equal, CB, AO.mult))
+    op("v", ["i3"], ["BN"], ts(T.BN[:], T.i3[:], 0.0, AO.is_equal, -CB, AO.mult))
+    half = (H - 0.5) * CB / BIG
+    op("v", ["i2"], ["HB0"], ts(T.HB[:, 0:NM], T.i2[:, 0:NM], 0.0, AO.mult, -half, AO.add))
+    op("v", ["i2"], ["HB1"], ts(T.HB[:, NM:2 * NM], T.i2[:, 0:NM], 0.0, AO.mult, half, AO.add))
+    op("v", ["i4"], ["MK"], ts(T.MK[:], T.i4[:], 0.0, AO.is_gt, -40.0, AO.mult))
+    op("v", ["b8"], ["cd"], ts(T.cd[:], T.b8[:], 1.0 / B, AO.mult))
+    op("v", ["I0f"], ["W0"], ts(T.W0[:], T.I0f[:], float(DUMP), AO.add))
+    op("v", ["MK"], ["MK"], ts(T.MK[:], T.MK[:], -half, AO.add))
+    op("v", ["cus"], ["gy"], tc(T.GB[:, GY:GY + Q], T.cus[:]))
+    op("v", ["I0f"], ["gw"], ts(T.GB[:, GY + Q:GW], T.I0f[:], float(DUMP - 4), AO.add))
+    for k in range(K):
+        c, q, o = OFF[k] // 16, SIZES[k] // 16, GO[k] + SIZES[k]
+        op("v", ["R0f"], [("Ru", k)], tc(T.Ru[:, QS * k:QS * k + q], T.R0f[:, c:c + q]))
+        op("v", ["I0f"], [("gr", k)], ts(T.GB[:, o:o + q], T.I0f[:, c:c + q], -3.0, AO.add))
+        if GO[k + 1] > o + q:
+            op("v", ["I0f"], [("gr", k)], tc(T.GB[:, o + q:GO[k + 1]], T.I0f[:, 0:GO[k + 1] - o - q]))
+
+    def turn(i):
+        s, k = divmod(i, K)
+        return s, k, SIZES[k], SIZES[k] // 16, s * M + OFF[k]
+
+    def cols(name, i):
+        s, k, n, q, o = turn(i)
+        return T[name][:, o:o + n]
+
+    def wide(name, i, a=0, b=None):
+        s, k, n, q, o = turn(i)
+        return T[name][:, 16 * (o + a):16 * (o + (n if b is None else b))]
+
+    def lasts(name, i):
+        s, k, n, q, o = turn(i)
+        return T[name][:, 16 * o + 15:16 * (o + n):16]
+
+    def came(i, a, b):
+        s, k, n, q, o = turn(i)
         if s == 0:
-            J, j0 = T.J0, OFF[k]
+            return T.I0[:, o + a:o + b]
+        h = HO[k] + (s - 1) * q
+        return (T.H1 if s == 1 else T.H2)[:, h + a:h + b]
+
+    def camekey(i):
+        return ("I0", i) if i < K else "aH%d" % i
+
+    def goes(i):
+        s, k, n, q, o = turn(i)
+        buf, h = (T.oH, HO[k]) if s == 0 else (T.H1, HO[k] + 2 * n + q)
+        return buf[:, h:h + n], buf[:, h + n:h + 2 * n], buf[:, h + 2 * n:h + 2 * n + q]
+
+    def piece(i, a):
+        o = turn(i)[4] + a * PIECE
+        return o, o // PIECE
+
+    def part(name, i, a, c0=0, c1=PIECE):
+        o = piece(i, a)[0]
+        return T[name][:, 16 * (o + c0):16 * (o + c1)]
+
+    def ends(name, i, a):
+        o = piece(i, a)[0]
+        return T[name][:, 16 * o + 15:16 * (o + PIECE):16]
+
+    def xb(j, h):
+        b = (HALVES * j + h) % XB
+        return ("x", b), 512 * b
+
+    def gathers(stage, i, a, R, out, win, lst):
+        o, j = piece(i, a)
+        na = PIECE - SHARE.get((stage, j), 0)
+        for q, c0, c1 in (("a", 0, na), ("v", na, PIECE)):
+            if c0 < c1:
+                gather(q, R, [(out, j, q)], part(out, i, a, c0, c1), win, lst[:, o + c0:o + c1])
+
+    def keys(name, j):
+        return [(name, j, q) for q in "av" if (name, j, q) in wrote]
+
+    def stJ(i):
+        if 0 < i < K:
+            first(i)
+
+    def stL(i, a):
+        gathers("L", i, a, [("J", i) if i < K else "aJ%d" % i, "L"], "A", T.L[:], T.J)
+
+    def stP(i, a):
+        j = piece(i, a)[1]
+        op("v", keys("A", j) + ["RM"], [("P", j)], scan(part("P", i, a), T.RM[:, 0:16 * PIECE], part("A", i, a)))
+
+    def half_of(name, i, a, h):
+        o = piece(i, a)[0]
+        return T[name][:, 16 * o + h:16 * (o + PIECE):HALVES]
+
+    def stX(i, a, h, tops):
+        j = piece(i, a)[1]
+        b, x = xb(j, h)
+        m = 16 // HALVES
+        w = m * PIECE
+        if not tops:
+            sums(("X", j, h), b, [(T.px[:, x:x + w], "NI", half_of("A", i, a, h), keys("A", j))], stop=False)
+        elif TURN_ON is None:
+            sums(("X", j, h), b, [(T.px[:, x + e:x + w:m], "PI", ends("P", i, a), [("P", j)]) for e in range(m)],
+                 start=False)
         else:
-            landed(("J", s, k), "aJ%d_%d" % (s, k))
-            J, j0 = T.J, s * M + OFF[k]
-        nv = (VL0 if s == 0 else VL)[k]
-        na = n - nv
-        if na:
-            gather("a", [("J", s, k), "L"], [("A", s, k, 0)], big("A", s, k, 0, na), T.L[:], J[:, j0:j0 + na])
-        if nv:
-            gather("v", [("J", s, k), "L"], [("A", s, k, 1)], big("A", s, k, na, n), T.L[:], J[:, j0 + na:j0 + n])
+            op("p", [("tT", i), "EX"], [("X", j, h)],
+               lambda: te.matmul(T.px[:, x:x + w], T.tT[0:PIECE, 128 * i:128 * i + 128], T.EX[0:PIECE, 0:w], False, True),
+               b, True)
 
-    def akeys(s, k):
-        return [("A", s, k, 0), ("A", s, k, 1)]
+    def stQ(i):
+        s, k, n, q, o = turn(i)
+        if TURN_ON is None:
+            return
+        b, tp, tT = ("a", T.pa, T.tT) if TURN_ON == "a" else ("m", T.pm, T.tT)
+        tp, tT = tp[0:n, 256:384], tT[0:n, 128 * i:128 * i + 128]
+        op("p", [("P", i), "ID"], [("tp", i)], lambda: te.matmul(tp, lasts("P", i), T.ID[:], True, True), b)
+        op(TURN_ON, [("tp", i)], [("tT", i)], tc(tT, tp) if TURN_ON == "v" else act(tT, tp, AF.Copy), b)
 
-    def stP(s, k):
-        n = SIZES[k]
-        op("v", akeys(s, k) + ["RM"], [("P", s, k)], scan(big("P", s, k), T.RM[:, 0:16 * n], big("A", s, k)))
-        for m in range(n // 32):
-            op("p", akeys(s, k) + ["NI"], [("X", s, k, m)],
-               mm(xb(k, m, 0, 512), T.NI[:], big("A", s, k, 32 * m, 32 * m + 32), True, False), [(k, m)])
-        op("p", [("P", s, k), "ID"], [("tp", s, k)], mm(T.tp[0:n, 0:128], lasts("P", s, k), T.ID[:]), ["tp"])
-        o = 128 * (s * K + k)
-        op("a", [("tp", s, k)], [("tT", s, k)], act(T.tT[0:n, o:o + 128], T.tp[0:n, 0:128]), ["tp"])
-        for m in range(n // 32):
-            op("p", [("tT", s, k), "EX"], [("X", s, k, m)],
-               mm(xb(k, m, 0, 512), T.tT[32 * m:32 * m + 32, o:o + 128], T.EX[32 * m:32 * m + 32, :], False, True),
-               [(k, m)])
+    def stV(i, a, h):
+        j = piece(i, a)[1]
+        b, x = xb(j, h)
+        op("v", keys("A", j) + [("X", j, h)], [("V", j, h)],
+           tt(half_of("V", i, a, h), T.px[:, x:x + 16 * PIECE // HALVES], half_of("A", i, a, h), AO.min), b)
 
-    def stV(s, k, m):
-        op("v", akeys(s, k) + [("X", s, k, m)], [("V", s, k, m)],
-           tt(big("V", s, k, 32 * m, 32 * m + 32), xb(k, m, 0, 512), big("A", s, k, 32 * m, 32 * m + 32), AO.min),
-           [(k, m)])
+    def stS(i, a):
+        j = piece(i, a)[1]
+        op("v", [("V", j, h) for h in range(HALVES)] + ["RM"], [("S", j)],
+           scan(part("S", i, a), T.RM[:, 0:16 * PIECE], part("V", i, a)))
 
-    def stS(s, k):
-        n = SIZES[k]
-        op("v", [("V", s, k, m) for m in range(n // 32)] + ["RM"], [("S", s, k)],
-           scan(big("S", s, k), T.RM[:, 0:16 * n], big("V", s, k)))
-        op("v", [("S", s, k)], [("su", s, k)], tc(sl("su", s, k), lasts("S", s, k)))
+    def stU(i, a):
+        o, j = piece(i, a)
+        op("v", [("S", j)], [("su", j)], tc(T.su[:, o:o + PIECE], ends("S", i, a)))
 
-    def stN(s, k):
-        n = SIZES[k]
-        q = n // 16
-        c0, c1 = cl(s, k)
-        if s > 0:
-            landed(("M", s, k), "aM%d_%d" % (s, k))
-        y, yk = place(s, k)
-        o = 24 * s + OFF[k] // 8
-        op("a", [yk], [("sg", s, k)], lambda: sc.activation(T.sg[:, o:o + q], y, AF.Sign, bias=-6.5))
-        op("a", [yk], [("sh", s, k)], lambda: sc.activation(T.sg[:, o + q:o + 2 * q], y, AF.Sign, bias=-7.5))
-        b = [(k, 1)]
-        p0 = 2 * n
-        N = ("N", s, k)
+    def verdicts(i, out):
+        s, k, n, q, o = turn(i)
+        return [(out, "NG", came(i, a, a + q), [camekey(i)]) for a in (2 * n, -q)[:s]]
+
+    def stD(i):
+        s, k, n, q, o = turn(i)
         if s == 0:
-            I, ik = ideal(s, k)
-            gk = ("gb", k)
-            op("p", [ik, "ID"], [N], mm(xb(k, 1, 0, n), T.ID[:], I, True, False), b)
-            op("p", [ik, "ID"], [N], mm(xb(k, 1, n, p0), T.ID[:], I, False, False), b)
-            op("p", [yk, "ID"], [N], mm(xb(k, 1, p0, p0 + q), T.ID[:], y, False, False), b)
-        else:
-            m = s * MT + MO[k]
-            gk = "GB%d" % s
-            if gk not in wrote:
-                landed(gk, "agap%d" % s)
-            op("p", [yk, "ID"], [N], mm(xb(k, 1, 0, p0 + q), T.ID[:], T.Ms[:, m:m + p0 + q], True, False), b)
-        op("p", [yk, "ID"], [N], mm(xb(k, 1, p0 + q, p0 + 2 * q), T.ID[:], y, False, False), b)
+            return
+        c = s * Q + OFF[k] // 16
+        y = T.pa[:, c:c + q]
+        gy = s * GW + GY + OFF[k] // 16
+        sums(("y", i), "a", [(y, "ID", T.GB[:, gy:gy + q], GAPS[s])] + verdicts(i, y))
+        op("a", [("y", i)], [("sg", i)], act(T.sg[:, c:c + q], y, AF.Sign, -6.5), "a")
+
+    def stN(i):
+        s, k, n, q, o = turn(i)
+        I, hk = came(i, 0, n), [camekey(i)]
+        x, b = 512 * (i % 2), ("n", i % 2)
         gs = s * GW + GO[k]
-        op("p", [gk, ("b5", k), ("b188", k)], [N],
-           mm(xb(k, 1, n, p0 + 2 * q), T.ID[:], T.GB[:, gs:gs + n + 2 * q], False, False), b)
-        op("p", [("sg", s, k), ("sh", s, k), "N4"], [N],
-           mm(xb(k, 1, p0, p0 + 2 * q), T.N4[:], T.sg[:, o:o + 2 * q], False, True), b)
-        op("v", [N], [("Ru", s, k)], tc(T.Ru[:, c0:c1], xb(k, 1, p0, p0 + q)), b)
-
-    def stG(s, k):
-        n = SIZES[k]
-        nv = VG[k]
-        na = n - nv
-        win = T.C[:, DUMP:DUMP + W]
-        o = s * M + OFF[k]
-        if na:
-            gather("a", [("su", s, k)] + allC, [("B", s, k, 0)], big("BB", s, k, 0, na), win, T.su[:, o:o + na])
-        if nv:
-            gather("v", [("su", s, k)] + allC, [("B", s, k, 1)], big("BB", s, k, na, n), win, T.su[:, o + na:o + n])
-
-    def stR(s, k):
-        c0, c1 = cl(s, k)
-        gather("a", [("Ru", s, k)] + allC, [("RR", s, k)], sl("RR", s, k), T.C[:, DUMP:DUMP + W], T.Ru[:, c0:c1])
-
-    def stZ(s, k):
-        n = SIZES[k]
-        In, GE = sl("In", s, k), sl("GE", s, k)
-        op("v", [("B", s, k, 0), ("B", s, k, 1), "RM"], [("Z", s, k)],
-           scan(big("Z", s, k), T.RM[:, 0:16 * n], big("BB", s, k)))
-        op("v", [("Z", s, k), ("N", s, k)], [("In", s, k)], tt(In, xb(k, 1, 0, n), lasts("Z", s, k), AO.max), [(k, 1)])
-        op("v", [("In", s, k), ("N", s, k)], [("GE", s, k)], tt(GE, In, xb(k, 1, n, 2 * n), AO.is_ge), [(k, 1)])
-        b = [(k, 0)]
-        op("p", ["BP", "HB0", "HB1"], [("+", s, k)],
-           mm(xb(k, 0, 0, 2 * n), T.BP[:], T.HB[:, NM - n:NM + n], True, False), b)
-        op("p", [("GE", s, k)], [("+", s, k)], mm(xb(k, 0, 0, n), T.BP[:], GE, False, False), b)
-        op("p", [("GE", s, k), "BN"], [("+", s, k)], mm(xb(k, 0, n, 2 * n), T.BN[:], GE, False, True), b)
-
-    def stF(s, k):
-        n = SIZES[k]
-        if s < ST - 1:
-            o = (s + 1) * MT + MO[k]
-            out, key = T.oMs[:, o:o + n], ("oI", s + 1, k)
+        ideals = [(T.pn[:, x:x + n], "ID", I, hk), (T.pn[:, x + n:x + 2 * n], "ID", I, hk)]
+        if s == 0:
+            terms = ideals + [(T.pn[:, x + n:x + 2 * n], "ID", T.GB[:, gs:gs + n], ["gg"])]
         else:
-            out, key = T.oF[:, OFF[k]:OFF[k] + n], ("oF", k)
-        b = [(k, 0)]
-        m1, m2 = sl("m1", s, k), xb(k, 0, 2 * n, 3 * n)
-        op("v", [("+", s, k), ("RR", s, k)], [("m1", s, k)], tt(m1, xb(k, 0, 0, n), sl("RR", s, k), AO.min), b)
-        op("v", [("+", s, k), ("In", s, k)], [("m2", s, k)], tt(m2, xb(k, 0, n, 2 * n), sl("In", s, k), AO.min), b)
-        op("v", [("m1", s, k), ("m2", s, k)], [key], tt(out, m2, m1, AO.max), b)
-        if s < ST - 1:
-            op("v", [key], [("oJ", s + 1, k)], tc(sl("oJ", s + 1, k), out))
-            push("oJ", "aJ%d_%d" % (s + 1, k), [("oJ", s + 1, k)])
-        else:
-            push("oF", "aF%d" % k, [key])
+            c = s * Q + OFF[k] // 16
+            both, lst = T.pn[:, x + n:x + 2 * n + q], T.pn[:, x + 2 * n:x + 2 * n + q]
+            terms = [(both, "ID", T.GB[:, gs:gs + n + q], GAPS[s])] + ideals
+            terms += [(both, "NG", came(i, n, 2 * n + q), hk)]
+            terms += verdicts(i, lst)[1:] + [(lst, "N4", T.sg[:, c:c + q], [("sg", i)])]
+        sums(("N", i), b, terms)
+        if s > 0:
+            op("v", [("N", i)], [("Ru", i)], tc(T.Ru[:, QS * i:QS * i + q], lst), b)
 
-    def stX(s, k):
-        n = SIZES[k]
-        q = n // 16
-        c = OFF[k] // 16
-        D, DS = sl("DD", s, k), sl("DS", s, k)
-        b0 = [(k, 0)]
-        op("v", [("+", s, k), "DM"], [("DD", s, k)], tt(D, xb(k, 0, 0, n), T.DM[:, OFF[k]:OFF[k] + n], AO.is_ge), b0)
-        if s < ST - 1:
-            o = (s + 1) * MT + MO[k]
-            m2 = xb(k, 0, 3 * n, 4 * n)
-            t, tk = base(s, k)
-            op("v", [("+", s, k), tk], [("m3", s, k)], tt(m2, xb(k, 0, n, 2 * n), t, AO.min), b0)
-        op("v", [("DD", s, k), "RM"], [("DS", s, k)], scan(DS, T.RM[:, 0:n], D))
-        if s < ST - 1:
-            op("v", [("m3", s, k), ("m1", s, k)], [("oT", s + 1, k)],
-               tt(T.oMs[:, o + n:o + 2 * n], m2, sl("m1", s, k), AO.max), b0)
-        y, yk = place(s, k)
-        os = s * M + OFF[k]
-        ls = T.DS[:, os + 15:os + n:16]
-        if s < ST - 1:
-            op("v", [("DS", s, k), yk], [("oy", s + 1, k)], tt(T.oMs[:, o + 2 * n:o + 2 * n + q], y, ls, AO.add))
-            push("oMs", "aM%d_%d" % (s + 1, k), [("oI", s + 1, k), ("oT", s + 1, k), ("oy", s + 1, k)])
-            op("v", [("DS", s, k), ("N", s, k)], [("wo", s, k)],
-               tt(T.wo[:, 12 * s + c:12 * s + c + q], xb(k, 1, 2 * n + q, 2 * n + 2 * q), ls, AO.mult), [(k, 1)])
-        else:
-            op("v", [("DS", s, k), yk], [("y", k)], tt(T.Ry[:, c:c + q], y, ls, AO.add))
+    def stR(i):
+        s, k, n, q, o = turn(i)
+        gather(RELOAD_ON, [("Ru", i)] + allC, [("RR", i)], cols("RR", i), T.C[:, DUMP:DUMP + W],
+               T.Ru[:, QS * i:QS * i + q])
 
-    def tail(s):
-        ks = range(K)
-        wo, ou = T.wo[:, 12 * s:12 * s + 12], T.ou[:, 12 * s:12 * s + 12]
-        op("v", [("wo", s, k) for k in ks] + ["cd"], [("wo", s)], tt(wo, wo, T.cd[:], AO.max))
-        op("v", [("wo", s)], [("ou", s)], tc(ou, wo))
-        op("v", [("ou", s)] + [("In", s, k) for k in ks], allC,
+    def stG(i, a):
+        gathers("G", i, a, [("su", piece(i, a)[1])] + allC, "BB", T.C[:, DUMP:DUMP + W], T.su)
+
+    def stZ(i, a):
+        j = piece(i, a)[1]
+        op("v", keys("BB", j) + ["RM"], [("Z", j)], scan(part("Z", i, a), T.RM[:, 0:16 * PIECE], part("BB", i, a)))
+
+    def stI(i):
+        s, k, n, q, o = turn(i)
+        x, b = 512 * (i % 2), ("n", i % 2)
+        zk = [("Z", piece(i, a)[1]) for a in range(n // PIECE)]
+        op("v", zk + [("N", i)], [("In", i)], tt(cols("In", i), T.pn[:, x:x + n], lasts("Z", i), AO.max), b)
+
+    def stE(i):
+        s, k, n, q, o = turn(i)
+        x, b = 512 * (i % 2), ("n", i % 2)
+        GE, gk = cols("GE", i), [("GE", i)]
+        op("v", [("In", i), ("N", i)], gk, tt(GE, cols("In", i), T.pn[:, x + n:x + 2 * n], AO.is_ge), b)
+        sums(("+", i), "y", [(T.py[:, 0:2 * n], "PI", T.HB[:, NM - n:NM + n], ["HB0", "HB1"]),
+                             (T.py[:, 0:n], "BP", GE, gk), (T.py[:, n:2 * n], "BN", GE, gk)])
+        sums(("m", i), "m", [(T.pm[:, 0:n], "PI", T.MK[:, 0:n], ["MK"]), (T.pm[:, 0:n], "BP", GE, gk)])
+
+    def stF(i):
+        s, k, n, q, o = turn(i)
+        out = goes(i)[0] if s < ST - 1 else T.oF[:, OFF[k]:OFF[k] + n]
+        m1 = T.py[:, 2 * n:3 * n]
+        op("v", [("+", i), ("RR", i)], [("m1", i)], tt(m1, T.py[:, 0:n], cols("RR", i), AO.min), "y")
+        op("v", [("+", i), ("In", i)], [("m2", i)], tt(cols("m2", i), T.py[:, n:2 * n], cols("In", i), AO.min), "y")
+        op("v", [("m1", i), ("m2", i)], [("oI", i)], tt(out, m1, cols("m2", i), AO.max), "y")
+        if s < ST - 1:
+            op("v", [("oI", i)], [("oJ", i)], tc(cols("oJ", i + K), out))
+            push("aJ%d" % (i + K), [("oJ", i)])
+        elif i < LAST:
+            push("aF%d" % k, [("oI", i)])
+
+    def stY(i):
+        s, k, n, q, o = turn(i)
+        op("v", [("m", i), "RM"], [("DS", i)], scan(cols("DS", i), T.RM[:, 0:n], T.pm[:, 0:n]), "m")
+
+    def stH(i):
+        s, k, n, q, o = turn(i)
+        if s == ST - 1:
+            return
+        oI, ou, orr = goes(i)
+        u, hk = T.pa[:, 64:64 + n], [camekey(i)]
+        terms = [(u, "NG", came(i, 0, n), hk)]
+        if s > 0:
+            terms.append((u, "ID", came(i, n, 2 * n), hk))
+        sums(("u", i), "a", terms + [(u, "ID", cols("m2", i), [("m2", i)])])
+        op("a", [("u", i)], [("ou", i)], act(ou, u, AF.Relu), "a")
+        op("a", [("DS", i)], [("or", i)], act(orr, T.DS[:, o + 15:o + n:16], AF.Sign, 0.0, -1.0))
+        push("aH%d" % (i + K), [("oI", i), ("ou", i), ("or", i)])
+        if i == 0:
+            push("aG2", GAPS[1])
+
+    def stW(i):
+        if i != 2 * K - 1:
+            return
+        op("a", [("y", j) for j in range(K, 2 * K)], ["sh"], act(T.sh[:], T.pa[:, Q:2 * Q], AF.Sign, -7.5), "a")
+        w = T.pm[:, 128:128 + Q]
+        terms = [(w, "ID", T.GB[:, GW + GY + Q:2 * GW], ["aG1_1"])]
+        for k in range(K):
+            c = 128 + OFF[k] // 16
+            terms += verdicts(K + k, T.pm[:, c:c + SIZES[k] // 16])
+        sums("W1", "m", terms + [(w, "N4", T.sh[:], ["sh"])])
+
+    def stT(i):
+        s = i // K
+        if i % K < K - 1 or s == ST - 1:
+            return
+        turns = range(s * K, s * K + K)
+        wo, ou = T["wo%d" % s][:], T.ou[:, Q * s:Q * s + Q]
+        ls = T.DS[:, s * M + 15:s * M + M:16]
+        dk = [("DS", j) for j in turns]
+        if s == 0:
+            op("v", dk + ["W0"], [("wo", s)], tt(wo, ls, T.W0[:], AO.min))
+        else:
+            op("v", dk + ["W1"], [("wo", s)], tt(wo, T.pm[:, 128:128 + Q], ls, AO.min), "m")
+        op("v", [("wo", s), "cd"], [("wo", s)], tt(wo, wo, T.cd[:], AO.max))
+        op("v", [("wo", s)], [("ou", s, 0)], tc(ou, wo))
+        op("v", [("ou", s, 0)] + [("In", j) for j in turns], allC,
            tc(T.C[:, 0:DUMP + W].indirect(ou), T.In[:, s * M:s * M + M]))
 
-    stages = {"L": stL, "P": stP, "V": stV, "S": stS, "N": stN, "G": stG, "R": stR, "Z": stZ, "F": stF, "X": stX,
-              "T": tail}
+    def stC(i):
+        if i > 0:
+            return
+        for k in range(K):
+            op("v", ["gaps"], ["gg"], tc(T.GB[:, GO[k]:GO[k] + SIZES[k]], T.gaps[:, OFF[k]:OFF[k] + SIZES[k]]),
+               None, True)
+        for h in range(2):
+            push("aG1_%d" % h, ["gg", "gy", "gw"] + [("gr", k) for k in range(K)])
 
-    for k in range(K):
-        first(k)
-        if k == 0:
-            stL(0, 0)
-            for kk in range(K):
-                op("v", ["gaps"], [("gb", kk)],
-                   tc(T.GB[:, GO[kk]:GO[kk] + SIZES[kk]], T.gaps[:, OFF[kk]:OFF[kk] + SIZES[kk]]))
-    push("GB", "agap1", [(x, k) for x in ("gb", "b5", "b188") for k in range(K)], GW)
-    landed("GB1", "agap1")
-    push("GB", "agap2", ["GB1"], GW)
-    for t in ORDER:
-        if t != "0L0":
-            stages[t[1]](int(t[0]), *[int(x) for x in t[2:]])
-    yk = [("y", k) for k in range(K)]
-    op("v", yk, ["oFq"], ts(T.oFq[:], T.Ry[:], 8.0, AO.is_ge, -8.0, AO.mult))
-    op("v", yk + ["oFq"], ["oFy"], tt(T.oFy[:], T.Ry[:], T.oFq[:], AO.add))
-    push("oFy", "aFy", ["oFy"])
+    def stO():
+        turns = range(2 * K, 3 * K)
+        op("v", [("DS", i) for i in turns], ["y1"], ts(T.y1[:], T.DS[:, 2 * M + 15:3 * M:16], 1.0, AO.min))
+        op("v", ["y1"] + [("y", i) for i in turns], ["y2"], tt(T.y2[:], T.pa[:, 2 * Q:3 * Q], T.y1[:], AO.add), "a")
+        op("v", ["y2"], ["y3"], ts(T.y3[:], T.y2[:], float(B), AO.is_ge, -float(B), AO.mult))
+        op("v", ["y2", "y3"], ["oFy"], tt(T.oF[:, M:M + Q], T.y2[:], T.y3[:], AO.add))
+        push("aF%d" % (K - 1), ["oFy", ("oI", LAST)])
+
+    stages = {"J": stJ, "D": stD, "N": stN, "R": stR, "E": stE, "F": stF, "Y": stY, "T": stT, "C": stC, "O": stO,
+              "I": stI, "H": stH, "t": stW, "q": stQ,
+              "L": stL, "P": stP, "S": stS, "U": stU, "G": stG, "Z": stZ,
+              "A": lambda i, a: stV(i, a, 0), "B": lambda i, a: stV(i, a, 1),
+              "n": lambda i, a: stX(i, a, 0, False), "o": lambda i, a: stX(i, a, 1, False),
+              "x": lambda i, a: stX(i, a, 0, True), "w": lambda i, a: stX(i, a, 1, True)}
+    for t in tokens(rank):
+        stages[t[0]](*[int(x) for x in t[1:].split(".") if x])
 
     total = 0
     for k in range(K):
-        landed(("F", k), "aF%d" % k)
-        wait("s", [wrote[("F", k)]])
-        g.sync.dma_start(T.yi[:, OFF[k]:OFF[k] + SIZES[k]], T.F[:, OFF[k]:OFF[k] + SIZES[k]]).then_inc(sem.st, 16)
+        wait("s", [wrote["aF%d" % k]])
+        g.sync.dma_start(T.yi[:, OFF[k]:OFF[k] + SIZES[k]], T["F%d" % k][:, 0:SIZES[k]]).then_inc(sem.st, 16)
         total += 16
-    landed("Fy", "aFy")
-    wait("s", [wrote["Fy"]])
-    g.sync.dma_start(T.yc[:], T.Fy[:]).then_inc(sem.st, 16)
+    wait("a", [wrote["aF%d" % (K - 1)]])
+    g.scalar.dma_start(T.yc[:], T["F%d" % (K - 1)][:, SIZES[-1]:SIZES[-1] + Q]).then_inc(sem.st, 16)
     total += 16
     g.sync.wait_ge(sem.st, total)
     g.wait_ge(sem.ls, sent[0])

@@ -7,31 +7,46 @@ OFF = [sum(SIZES[:k]) for k in range(K)]
 NM = max(SIZES)
 Q = M // 16
 QS = 2 * -(-NM // 32)
-DUMP = M
+DUMP = W + 8
 BIG = 2048.0
 CB = 2 * BIG
 LAST = ST * K - 1
-SHARE = {("L", 1): 32, ("G", 17): 32}
-RELOAD_ON = "a"
-TURN_ON = None
 PIECE = 32
-HALVES = 1
-XB = 3
+XB = 4
+WIDE = {}
+SHARE = [("L", 1), ("G", 17)]
+PER = 1
+WRITES = [K - 1]
 
-_R = ("P1.0 n1.0 S0.1 U0.1 J2 L1.1 N0 G0.0 G0.1 H-1 P1.1 x1.0 Z0.0 n1.1 A1.0 Z0.1 I0 x1.1 C1 R0 S1.0 t0 L2.0 D1 E0 U1.0 "
-      "A1.1 F0 Y0 T0")
+_R = ("P1.0 j2 G0.0 S0.1 U0.1 J2 x1.0 u0 P1.1 G0.1 D1 Z0.0 r-1 C1 A1.0 t0 g-1 Z0.1 H-1 Y-1 x1.1 N1 d1 I0 E0 w0 R0 S1.0 M1 "
+      "e0 L2.0 l0 U1.0 A1.1 F0 c0 n2.0 T0 L2.1 h0 n2.1")
 ROUND = {False: _R, True: _R}
+HEAD = ("L0.1 J1 L0.0 L1.0 P0.0 P0.1 C0 n0.0 P1.0 n0.1 j2 x0.0 A0.0 S0.0 U0.0 R0 x0.1 A0.1 j1 n1.0 N0 S0.1 U0.1 L1.1 P1.1 "
+        "x1.0 J2 A1.0 n1.1 N1 G0.0 Z0.0 x1.1 S1.0 G0.1 Z0.1 I0 E0 e0 U1.0 l0 A1.1 F0 L2.0 P2.0 h0 n2.0 L2.1 S1.1 N2 U1.1 "
+        "P2.1 G1.0 Z1.0 H0 r0 R1 x2.0 n2.1 A2.0 S2.0 G1.1 Z1.1 I1 E1 x2.1 A2.1 U2.0 e1 l1 Y0 L3.0 g0 F1 n3.0")
+TAIL = ("x7.1 A7.0 Z6.1 S7.0 H5 I6 Y5 A7.1 d7 L8.0 L8.1 E6 N7 P8.0 M7 R6 n8.0 U7.0 G7.0 S7.1 u7 U7.1 P8.1 e6 F6 G7.1 x8.0 "
+        "n8.1 A8.0 Z7.0 x8.1 S8.0 N8 A8.1 U8.0 D8 Z7.1 S8.1 I7 d8 U8.1 M8 E7 e7 G8.1 G8.0 Z8.0 R7 Z8.1 F7 l7 I8 E8 l6 e8 "
+        "u8 l8 R8 F8 O")
+
+
+def exists(stage, i, a):
+    s, k = divmod(i, K)
+    if not 0 <= i <= LAST or a * WIDE.get(stage, 1) * PIECE >= SIZES[k]:
+        return False
+    return {"J": 0 < i < K, "j": 0 < i < K, "C": i == 0, "g": i == 0, "t": i == 2 * K - 1, "w": i == 2 * K - 1,
+            "c": k in WRITES and s < 2, "T": k in WRITES and s < 2}.get(
+        stage, s > 0 if stage in "DdMu" else s < 2 if stage in "hHrY" else True)
 
 
 def order(stages):
     out = []
-    for t in range(-4, LAST + 4):
+    for t in range(-4 * PER, LAST + 4 * PER, PER):
         for x in stages.split():
-            i, _, a = x[1:].partition(".")
-            i = t + int(i)
-            if 0 <= i <= LAST:
-                out.append(x[0] + str(i) + ("." + (a or "0") if x[0] in "LPSUGZABnoxw" else ""))
-    return out + ["O"]
+            i, dot, a = x[1:].partition(".")
+            if exists(x[0], t + int(i), int(a or 0)):
+                out.append(x[0] + str(t + int(i)) + dot + a)
+    head, tail = HEAD.split(), TAIL.split()
+    return head + [t for t in out if t not in head and t not in tail] + tail
 
 
 ORDERS = {r: order(ROUND[r]) for r in ROUND}
@@ -41,9 +56,7 @@ def pad8(x):
     return -(-x // 8) * 8
 
 
-GO = [sum(pad8(n + n // 16) for n in SIZES[:k]) for k in range(K + 1)]
-GY = GO[K]
-GW = GY + 2 * Q
+GW = M + 2 * Q
 HO = [sum(pad8(4 * n + n // 8) for n in SIZES[:k]) for k in range(K + 1)]
 SCRATCH = {
     "C": ("sbuf", [128, DUMP + W], "int32"),
@@ -53,13 +66,9 @@ SCRATCH = {
     "GB": ("sbuf", [128, ST * GW], "float16"),
     "RM": ("sbuf", [128, 16 * NM], "bfloat16"),
     "HB": ("sbuf", [128, 2 * NM], "float16"),
-    "MK": ("sbuf", [128, NM], "float16"),
-    "EX": ("sbuf", [128, 8 * NM], "float16"),
-    "tT": ("sbuf", [128, ST * K * 128], "float16"),
-    "i1": ("sbuf", [128, 8 * NM], "int32"),
-    "i2": ("sbuf", [128, 128], "int32"),
+    "UW": ("sbuf", [128, 144], "float16"),
+    "i2": ("sbuf", [128, 144], "int32"),
     "i3": ("sbuf", [128, 128], "int32"),
-    "i4": ("sbuf", [128, NM], "int32"),
     "I0": ("sbuf", [128, M], "float16"),
     "Ru": ("sbuf", [128, ST * K * QS], "uint16"),
     "sg": ("sbuf", [128, ST * Q], "float16"),
@@ -72,24 +81,22 @@ SCRATCH = {
     "H1": ("sbuf", [128, HO[K]], "float16"),
     "H2": ("sbuf", [128, HO[K]], "float16"),
     "oF": ("sbuf", [128, M + Q], "float32"),
-    "px": ("psum", [128, 3 * 512], "float32"),
+    "px": ("psum", [128, XB * 512], "float32"),
     "pn": ("psum", [128, 2 * 512], "float32"),
     "py": ("psum", [128, 512], "float32"),
-    "pm": ("psum", [128, 512], "float32"),
     "pa": ("psum", [128, 512], "float32"),
 }
 for _k in range(K):
     SCRATCH["F%d" % _k] = ("dram", [128, SIZES[_k] + Q * (_k == K - 1)], "float32")
-for _n in ("ID", "NG", "NI", "PI", "N4", "BP", "BN"):
+for _n in ("ID", "NG", "NI", "PI", "N4", "HF", "BP", "BN"):
     SCRATCH[_n] = ("sbuf", [128, 128], "float16")
 for _n in ("i5", "i6", "i7"):
     SCRATCH[_n] = ("sbuf", [128, Q], "int32")
-for _n in ("b8", "cd", "I0f", "R0f", "W0", "wo0", "wo1", "y1", "y2", "y3"):
+for _n in ("b8", "pm", "I0f", "R0f", "X0", "rc0", "rc1", "wo0", "wo1", "y1", "y2", "y3"):
     SCRATCH[_n] = ("sbuf", [128, Q], "float32")
 for _n in ("A", "V", "P", "S", "BB", "Z"):
     SCRATCH[_n] = ("sbuf", [128, ST * M * 16], "float16")
-for _n, _d in (("su", "uint16"), ("RR", "float16"), ("In", "float16"), ("GE", "float16"), ("m2", "float16"),
-               ("DS", "float16")):
+for _n, _d in (("su", "uint16"), ("RR", "float16"), ("In", "float16"), ("GE", "float16"), ("m2", "float16")):
     SCRATCH[_n] = ("sbuf", [128, ST * M], _d)
 SEMAPHORES = ["v", "a", "p", "gq", "ls", "lcu", "lla", "lgap", "st", "aG1_0", "aG1_1", "aG2"]
 SEMAPHORES += ["lck%d" % _k for _k in range(K)]
@@ -111,15 +118,15 @@ for _k in range(K):
 def issue(tokens):
     out = []
     for t in tokens:
-        i = int(t[1:]) if t[0] in "FH" else None
-        if t == "C0":
-            out += ["aG1_0", "aG1_1"]
+        i = int(t[1:]) if t[0] in "FY" else None
+        if t[0] == "C":
+            out += GAPS[1]
+        elif t[0] == "g":
+            out += GAPS[2]
         elif t[0] == "F" and i < LAST:
             out.append("aJ%d" % (i + K) if i < 2 * K else "aF%d" % (i - 2 * K))
-        elif t[0] == "H" and i < 2 * K:
+        elif t[0] == "Y":
             out.append("aH%d" % (i + K))
-            if i == 0:
-                out.append("aG2")
         elif t == "O":
             out.append("aF%d" % (K - 1))
     return out
@@ -236,16 +243,14 @@ def rank_program(g, core, T, topo):
     def tc(out, in_):
         return lambda: v.tensor_copy(out, in_)
 
-    def scan(out, mask, data):
-        return lambda: v.tensor_tensor_scan(out, mask, data, 0.0, AO.mult, AO.max)
-
-    def act(out, in_, fn, bias=0.0, scale=1.0):
-        return lambda: sc.activation(out, in_, fn, bias=bias, scale=scale)
+    def act(out, in_, fn, bias=0.0):
+        return lambda: sc.activation(out, in_, fn, bias=bias)
 
     def sums(key, bank, terms, start=True, stop=True):
         for j, (out, wt, rhs, R) in enumerate(terms):
             first, last = start and j == 0, stop and j == len(terms) - 1
-            op("p", R + [wt], [key], lambda: te.matmul(out, T[wt][:], rhs, first, last), bank, not first)
+            name, c = wt if isinstance(wt, tuple) else (wt, 0)
+            op("p", R + [name], [key], lambda: te.matmul(out, T[name][:, c:c + 128], rhs, first, last), bank, not first)
 
     def gather(q, R, Wk, out, win, off):
         op(q, R, Wk, tc(out, win.indirect(off)) if q == "v" else lambda: sc.activation(out, win.indirect(off), AF.Copy))
@@ -259,57 +264,46 @@ def rank_program(g, core, T, topo):
     load(g.sync, "gaps", "lgap", T.gaps[:], T.gap[:])
     allC = [("C", k) for k in range(K)]
 
+    def first(k, q):
+        o, n = OFF[k], SIZES[k]
+        name = "J" if q == "v" else "I0"
+        gather(q, [("I0u", k)] + allC[:k + 1], [(name, k)], T[name][:, o:o + n], T.C[:, DUMP:DUMP + 8 * (o + n)],
+               T.I0u[:, QS * k:QS * k + n // 16])
+
     op("g", [], ["i5"], lambda: g.iota(T.i5[:], [[0, Q]], 0, 8))
     op("g", [], ["i6"], lambda: g.iota(T.i6[:], [[128, Q]], 0, 0))
-    op("g", [], ["i2"], lambda: g.iota(T.i2[:], [[1, 128]], 0, -1))
-    if TURN_ON:
-        op("g", [], ["i1"], lambda: g.iota(T.i1[:], [[1, 8 * NM]], 0, -8))
+    op("g", [], ["i2"], lambda: g.iota(T.i2[:], [[1, 144]], 0, -1))
     op("g", [], ["i3"], lambda: g.iota(T.i3[:], [[16, 8], [0, 16]], 15, -1))
-    op("g", [], ["i4"], lambda: g.iota(T.i4[:], [[1, NM]], 0, -1))
 
     op("v", [], ["RM"], lambda: v.memset(T.RM[:], 1.0))
     op("v", ["i5"], ["i5"], ts(T.i5[:], T.i5[:], 127, AO.bitwise_and))
     op("v", [], ["RM"], lambda: v.memset(T.RM[:, 0:16 * NM:16], 0.0))
     op("v", ["i5", "i6"], ["b8"], tt(T.b8[:], T.i5[:], T.i6[:], AO.add))
-    for name, wt in (("ID", 1.0), ("NI", -BIG), ("PI", BIG), ("NG", -1.0), ("N4", -4.0)):
-        op("v", ["i2"], [name], ts(T[name][:], T.i2[:], 0.0, AO.is_equal, wt, AO.mult))
+    op("v", ["i5"], ["pm"], ts(T.pm[:], T.i5[:], -1.0 / B, AO.mult, 15.0, AO.add))
+    for name, wt in (("ID", 1.0), ("NI", -BIG), ("PI", BIG), ("NG", -1.0), ("N4", -4.0), ("HF", 0.5)):
+        op("v", ["i2"], [name], ts(T[name][:], T.i2[:, 0:128], 0.0, AO.is_equal, wt, AO.mult))
     op("v", ["b8", "cus"], ["I0f"], tt(T.I0f[:], T.b8[:], T.cus[:], AO.add))
     op("v", ["cus"], ["i7"], ts(T.i7[:], T.cus[:], 1.0, AO.add))
     for k in range(K):
         c, q = OFF[k] // 16, SIZES[k] // 16
         op("v", ["I0f"], [("I0u", k)], tc(T.I0u[:, QS * k:QS * k + q], T.I0f[:, c:c + q]))
-
-    def first(k):
-        o, n = OFF[k], SIZES[k]
-        win, off = T.C[:, DUMP:DUMP + 8 * (o + n)], T.I0u[:, QS * k:QS * k + n // 16]
-        gather("v", [("I0u", k)] + allC[:k + 1], [("J", k)], T.J[:, o:o + n], win, off)
-        gather("a", [("I0u", k)] + allC[:k + 1], [("I0", k)], T.I0[:, o:o + n], win, off)
-
     op("v", ["i7"], ["i7"], ts(T.i7[:], T.i7[:], B - 1, AO.bitwise_and))
     op("v", ["i3"], ["i3"], ts(T.i3[:], T.i3[:], 4, AO.arith_shift_right))
-    first(0)
-    if TURN_ON:
-        op("v", ["i1"], ["i1"], ts(T.i1[:], T.i1[:], 2047, AO.bitwise_and))
-        op("v", ["i1"], ["EX"], ts(T.EX[:], T.i1[:], 8.0, AO.is_lt, BIG, AO.mult))
-    op("v", ["i4"], ["i4"], ts(T.i4[:], T.i4[:], 15, AO.bitwise_and))
+    first(0, "v")
+    first(0, "a")
     op("v", ["b8", "i7"], ["R0f"], tt(T.R0f[:], T.b8[:], T.i7[:], AO.add))
     op("v", ["i3"], ["BP"], ts(T.BP[:], T.i3[:], 0.0, AO.is_equal, CB, AO.mult))
     op("v", ["i3"], ["BN"], ts(T.BN[:], T.i3[:], 0.0, AO.is_equal, -CB, AO.mult))
+    op("v", ["i2", "pm"], ["UW"], ts(T.UW[:], T.i2[:], T.pm[:, 0:1], AO.is_equal, CB, AO.mult))
     half = (H - 0.5) * CB / BIG
     op("v", ["i2"], ["HB0"], ts(T.HB[:, 0:NM], T.i2[:, 0:NM], 0.0, AO.mult, -half, AO.add))
     op("v", ["i2"], ["HB1"], ts(T.HB[:, NM:2 * NM], T.i2[:, 0:NM], 0.0, AO.mult, half, AO.add))
-    op("v", ["i4"], ["MK"], ts(T.MK[:], T.i4[:], 0.0, AO.is_gt, -40.0, AO.mult))
-    op("v", ["b8"], ["cd"], ts(T.cd[:], T.b8[:], 1.0 / B, AO.mult))
-    op("v", ["I0f"], ["W0"], ts(T.W0[:], T.I0f[:], float(DUMP), AO.add))
-    op("v", ["MK"], ["MK"], ts(T.MK[:], T.MK[:], -half, AO.add))
-    op("v", ["cus"], ["gy"], tc(T.GB[:, GY:GY + Q], T.cus[:]))
-    op("v", ["I0f"], ["gw"], ts(T.GB[:, GY + Q:GW], T.I0f[:], float(DUMP - 4), AO.add))
+    op("v", ["I0f"], ["X0"], ts(T.X0[:], T.I0f[:], 0.5, AO.add))
+    op("v", ["cus"], ["gy"], tc(T.GB[:, M:M + Q], T.cus[:]))
+    op("v", ["I0f"], ["gr"], ts(T.GB[:, M + Q:GW], T.I0f[:], -3.0, AO.add))
     for k in range(K):
-        c, q, o = OFF[k] // 16, SIZES[k] // 16, GO[k] + SIZES[k]
+        c, q = OFF[k] // 16, SIZES[k] // 16
         op("v", ["R0f"], [("Ru", k)], tc(T.Ru[:, QS * k:QS * k + q], T.R0f[:, c:c + q]))
-        op("v", ["I0f"], [("gr", k)], ts(T.GB[:, o:o + q], T.I0f[:, c:c + q], -3.0, AO.add))
-        if GO[k + 1] > o + q:
-            op("v", ["I0f"], [("gr", k)], tc(T.GB[:, o + q:GO[k + 1]], T.I0f[:, 0:GO[k + 1] - o - q]))
 
     def turn(i):
         s, k = divmod(i, K)
@@ -319,13 +313,9 @@ def rank_program(g, core, T, topo):
         s, k, n, q, o = turn(i)
         return T[name][:, o:o + n]
 
-    def wide(name, i, a=0, b=None):
+    def lists(name, i, at=0):
         s, k, n, q, o = turn(i)
-        return T[name][:, 16 * (o + a):16 * (o + (n if b is None else b))]
-
-    def lasts(name, i):
-        s, k, n, q, o = turn(i)
-        return T[name][:, 16 * o + 15:16 * (o + n):16]
+        return T[name][:, at + o // 16:at + o // 16 + q]
 
     def came(i, a, b):
         s, k, n, q, o = turn(i)
@@ -335,151 +325,130 @@ def rank_program(g, core, T, topo):
         return (T.H1 if s == 1 else T.H2)[:, h + a:h + b]
 
     def camekey(i):
-        return ("I0", i) if i < K else "aH%d" % i
+        return [("I0", i) if i < K else "aH%d" % i]
 
     def goes(i):
         s, k, n, q, o = turn(i)
         buf, h = (T.oH, HO[k]) if s == 0 else (T.H1, HO[k] + 2 * n + q)
         return buf[:, h:h + n], buf[:, h + n:h + 2 * n], buf[:, h + 2 * n:h + 2 * n + q]
 
-    def piece(i, a):
-        o = turn(i)[4] + a * PIECE
-        return o, o // PIECE
+    def span(stage, i, a):
+        s, k, n, q, o = turn(i)
+        w = WIDE.get(stage, 1) * PIECE
+        w, o = min(w, n - a * w), o + a * w
+        return o, w, range(o // PIECE, (o + w) // PIECE)
 
-    def part(name, i, a, c0=0, c1=PIECE):
-        o = piece(i, a)[0]
-        return T[name][:, 16 * (o + c0):16 * (o + c1)]
+    def wide(name, o, w):
+        return T[name][:, 16 * o:16 * (o + w)]
 
-    def ends(name, i, a):
-        o = piece(i, a)[0]
-        return T[name][:, 16 * o + 15:16 * (o + PIECE):16]
+    def ends(name, o, w):
+        return T[name][:, 16 * o + 15:16 * (o + w):16]
 
-    def xb(j, h):
-        b = (HALVES * j + h) % XB
-        return ("x", b), 512 * b
+    def keys(name, js):
+        return [(name, j) for j in js]
 
     def gathers(stage, i, a, R, out, win, lst):
-        o, j = piece(i, a)
-        na = PIECE - SHARE.get((stage, j), 0)
-        for q, c0, c1 in (("a", 0, na), ("v", na, PIECE)):
-            if c0 < c1:
-                gather(q, R, [(out, j, q)], part(out, i, a, c0, c1), win, lst[:, o + c0:o + c1])
+        o, w, js = span(stage, i, a)
+        gather("v" if (stage, js[0]) in SHARE else "a", R, keys(out, js), wide(out, o, w), win, lst[:, o:o + w])
 
-    def keys(name, j):
-        return [(name, j, q) for q in "av" if (name, j, q) in wrote]
-
-    def stJ(i):
-        if 0 < i < K:
-            first(i)
+    def running(stage, i, a, out, src):
+        o, w, js = span(stage, i, a)
+        op("v", keys(src, js) + ["RM"], keys(out, js),
+           lambda: v.tensor_tensor_scan(wide(out, o, w), T.RM[:, 0:16 * w], wide(src, o, w), 0.0, AO.mult, AO.max))
 
     def stL(i, a):
         gathers("L", i, a, [("J", i) if i < K else "aJ%d" % i, "L"], "A", T.L[:], T.J)
 
-    def stP(i, a):
-        j = piece(i, a)[1]
-        op("v", keys("A", j) + ["RM"], [("P", j)], scan(part("P", i, a), T.RM[:, 0:16 * PIECE], part("A", i, a)))
-
-    def half_of(name, i, a, h):
-        o = piece(i, a)[0]
-        return T[name][:, 16 * o + h:16 * (o + PIECE):HALVES]
-
-    def stX(i, a, h, tops):
-        j = piece(i, a)[1]
-        b, x = xb(j, h)
-        m = 16 // HALVES
-        w = m * PIECE
+    def stX(i, a, tops):
+        o, w, (j,) = span("A", i, a)
+        b, x = ("x", j % XB), 512 * (j % XB)
         if not tops:
-            sums(("X", j, h), b, [(T.px[:, x:x + w], "NI", half_of("A", i, a, h), keys("A", j))], stop=False)
-        elif TURN_ON is None:
-            sums(("X", j, h), b, [(T.px[:, x + e:x + w:m], "PI", ends("P", i, a), [("P", j)]) for e in range(m)],
-                 start=False)
+            sums(("X", j), b, [(T.px[:, x:x + 512], "NI", wide("A", o, w), [("A", j)])], stop=False)
         else:
-            op("p", [("tT", i), "EX"], [("X", j, h)],
-               lambda: te.matmul(T.px[:, x:x + w], T.tT[0:PIECE, 128 * i:128 * i + 128], T.EX[0:PIECE, 0:w], False, True),
-               b, True)
+            sums(("X", j), b, [(T.px[:, x + e:x + 512:16], "PI", ends("P", o, w), [("P", j)]) for e in range(16)],
+                 start=False)
 
-    def stQ(i):
-        s, k, n, q, o = turn(i)
-        if TURN_ON is None:
-            return
-        b, tp, tT = ("a", T.pa, T.tT) if TURN_ON == "a" else ("m", T.pm, T.tT)
-        tp, tT = tp[0:n, 256:384], tT[0:n, 128 * i:128 * i + 128]
-        op("p", [("P", i), "ID"], [("tp", i)], lambda: te.matmul(tp, lasts("P", i), T.ID[:], True, True), b)
-        op(TURN_ON, [("tp", i)], [("tT", i)], tc(tT, tp) if TURN_ON == "v" else act(tT, tp, AF.Copy), b)
-
-    def stV(i, a, h):
-        j = piece(i, a)[1]
-        b, x = xb(j, h)
-        op("v", keys("A", j) + [("X", j, h)], [("V", j, h)],
-           tt(half_of("V", i, a, h), T.px[:, x:x + 16 * PIECE // HALVES], half_of("A", i, a, h), AO.min), b)
-
-    def stS(i, a):
-        j = piece(i, a)[1]
-        op("v", [("V", j, h) for h in range(HALVES)] + ["RM"], [("S", j)],
-           scan(part("S", i, a), T.RM[:, 0:16 * PIECE], part("V", i, a)))
+    def stA(i, a):
+        o, w, (j,) = span("A", i, a)
+        b, x = ("x", j % XB), 512 * (j % XB)
+        op("v", [("A", j), ("X", j)], [("V", j)], tt(wide("V", o, w), T.px[:, x:x + 512], wide("A", o, w), AO.min), b)
 
     def stU(i, a):
-        o, j = piece(i, a)
-        op("v", [("S", j)], [("su", j)], tc(T.su[:, o:o + PIECE], ends("S", i, a)))
+        o, w, js = span("U", i, a)
+        op("v", keys("S", js), keys("su", js), tc(T.su[:, o:o + w], ends("S", o, w)))
+
+    def stG(i, a):
+        gathers("G", i, a, keys("su", span("G", i, a)[2]) + allC, "BB", T.C[:, DUMP:DUMP + W], T.su)
 
     def verdicts(i, out):
         s, k, n, q, o = turn(i)
-        return [(out, "NG", came(i, a, a + q), [camekey(i)]) for a in (2 * n, -q)[:s]]
+        return [(out, "HF", came(i, a, a + q), camekey(i)) for a in (2 * n, -q)[:s]]
+
+    def ahead(i, part):
+        s, k, n, q, o = turn(i)
+        c = s * GW + M + part * Q + OFF[k] // 16
+        return T.GB[:, c:c + q]
 
     def stD(i):
-        s, k, n, q, o = turn(i)
-        if s == 0:
-            return
-        c = s * Q + OFF[k] // 16
-        y = T.pa[:, c:c + q]
-        gy = s * GW + GY + OFF[k] // 16
-        sums(("y", i), "a", [(y, "ID", T.GB[:, gy:gy + q], GAPS[s])] + verdicts(i, y))
-        op("a", [("y", i)], [("sg", i)], act(T.sg[:, c:c + q], y, AF.Sign, -6.5), "a")
+        y = lists("pa", i)
+        sums(("y", i), "a", [(y, "ID", ahead(i, 0), GAPS[i // K])] + verdicts(i, y))
+
+    def std(i):
+        op("a", [("y", i)], [("sg", i)], act(lists("sg", i), lists("pa", i), AF.Sign, i // K / 2 - 6.5), "a")
+
+    def nbank(i):
+        return 512 * (i % 2), ("n", i % 2)
 
     def stN(i):
         s, k, n, q, o = turn(i)
-        I, hk = came(i, 0, n), [camekey(i)]
-        x, b = 512 * (i % 2), ("n", i % 2)
-        gs = s * GW + GO[k]
-        ideals = [(T.pn[:, x:x + n], "ID", I, hk), (T.pn[:, x + n:x + 2 * n], "ID", I, hk)]
-        if s == 0:
-            terms = ideals + [(T.pn[:, x + n:x + 2 * n], "ID", T.GB[:, gs:gs + n], ["gg"])]
-        else:
-            c = s * Q + OFF[k] // 16
-            both, lst = T.pn[:, x + n:x + 2 * n + q], T.pn[:, x + 2 * n:x + 2 * n + q]
-            terms = [(both, "ID", T.GB[:, gs:gs + n + q], GAPS[s])] + ideals
-            terms += [(both, "NG", came(i, n, 2 * n + q), hk)]
-            terms += verdicts(i, lst)[1:] + [(lst, "N4", T.sg[:, c:c + q], [("sg", i)])]
-        sums(("N", i), b, terms)
+        I, hk = came(i, 0, n), camekey(i)
+        x, b = nbank(i)
+        bound = T.pn[:, x + n:x + 2 * n]
+        terms = [(T.pn[:, x:x + n], "ID", I, hk), (bound, "ID", I, hk),
+                 (bound, "ID", T.GB[:, s * GW + OFF[k]:s * GW + OFF[k] + n], GAPS[s])]
         if s > 0:
-            op("v", [("N", i)], [("Ru", i)], tc(T.Ru[:, QS * i:QS * i + q], lst), b)
+            terms.append((bound, "NG", came(i, n, 2 * n), hk))
+        sums(("N", i), b, terms)
+
+    def stM(i):
+        s, k, n, q, o = turn(i)
+        x, b = nbank(i)
+        lst = T.pn[:, x + 256:x + 256 + q]
+        sums(("M", i), b, [(lst, "ID", ahead(i, 1), GAPS[s])] + verdicts(i, lst) +
+             [(lst, "N4", lists("sg", i), [("sg", i)])])
+
+    def stu(i):
+        s, k, n, q, o = turn(i)
+        x, b = nbank(i)
+        op("v", [("M", i)], [("Ru", i)], ts(T.Ru[:, QS * i:QS * i + q], T.pn[:, x + 256:x + 256 + q], s / 2, AO.add), b)
 
     def stR(i):
         s, k, n, q, o = turn(i)
-        gather(RELOAD_ON, [("Ru", i)] + allC, [("RR", i)], cols("RR", i), T.C[:, DUMP:DUMP + W],
-               T.Ru[:, QS * i:QS * i + q])
-
-    def stG(i, a):
-        gathers("G", i, a, [("su", piece(i, a)[1])] + allC, "BB", T.C[:, DUMP:DUMP + W], T.su)
-
-    def stZ(i, a):
-        j = piece(i, a)[1]
-        op("v", keys("BB", j) + ["RM"], [("Z", j)], scan(part("Z", i, a), T.RM[:, 0:16 * PIECE], part("BB", i, a)))
+        gather("v" if ("R", i) in SHARE else "a", [("Ru", i)] + allC, [("RR", i)], cols("RR", i), T.C[:, DUMP:DUMP + W], T.Ru[:, QS * i:QS * i + q])
 
     def stI(i):
         s, k, n, q, o = turn(i)
-        x, b = 512 * (i % 2), ("n", i % 2)
-        zk = [("Z", piece(i, a)[1]) for a in range(n // PIECE)]
-        op("v", zk + [("N", i)], [("In", i)], tt(cols("In", i), T.pn[:, x:x + n], lasts("Z", i), AO.max), b)
+        x, b = nbank(i)
+        zk = keys("Z", range(o // PIECE, (o + n) // PIECE))
+        op("v", zk + [("N", i)], [("In", i)], tt(cols("In", i), T.pn[:, x:x + n], ends("Z", o, n), AO.max), b)
 
     def stE(i):
         s, k, n, q, o = turn(i)
-        x, b = 512 * (i % 2), ("n", i % 2)
+        x, b = nbank(i)
+        op("v", [("In", i), ("N", i)], [("GE", i)],
+           tt(cols("GE", i), cols("In", i), T.pn[:, x + n:x + 2 * n], AO.is_ge), b)
+
+    def ste(i):
+        s, k, n, q, o = turn(i)
         GE, gk = cols("GE", i), [("GE", i)]
-        op("v", [("In", i), ("N", i)], gk, tt(GE, cols("In", i), T.pn[:, x + n:x + 2 * n], AO.is_ge), b)
         sums(("+", i), "y", [(T.py[:, 0:2 * n], "PI", T.HB[:, NM - n:NM + n], ["HB0", "HB1"]),
                              (T.py[:, 0:n], "BP", GE, gk), (T.py[:, n:2 * n], "BN", GE, gk)])
-        sums(("m", i), "m", [(T.pm[:, 0:n], "PI", T.MK[:, 0:n], ["MK"]), (T.pm[:, 0:n], "BP", GE, gk)])
+
+    def stl(i):
+        s, k, n, q, o = turn(i)
+        out = lists("pa", i, 192)
+        sums(("l", i), "a", [(out, "PI", T.HB[:, 0:q], ["HB0"])] +
+             [(out, ("UW", 15 - e), T.GE[:, o + e:o + n:16], [("GE", i)]) for e in range(16)])
 
     def stF(i):
         s, k, n, q, o = turn(i)
@@ -494,77 +463,79 @@ def rank_program(g, core, T, topo):
         elif i < LAST:
             push("aF%d" % k, [("oI", i)])
 
-    def stY(i):
+    def sth(i):
         s, k, n, q, o = turn(i)
-        op("v", [("m", i), "RM"], [("DS", i)], scan(cols("DS", i), T.RM[:, 0:n], T.pm[:, 0:n]), "m")
-
-    def stH(i):
-        s, k, n, q, o = turn(i)
-        if s == ST - 1:
-            return
-        oI, ou, orr = goes(i)
-        u, hk = T.pa[:, 64:64 + n], [camekey(i)]
+        u, hk = T.pa[:, 64:64 + n], camekey(i)
         terms = [(u, "NG", came(i, 0, n), hk)]
         if s > 0:
             terms.append((u, "ID", came(i, n, 2 * n), hk))
         sums(("u", i), "a", terms + [(u, "ID", cols("m2", i), [("m2", i)])])
-        op("a", [("u", i)], [("ou", i)], act(ou, u, AF.Relu), "a")
-        op("a", [("DS", i)], [("or", i)], act(orr, T.DS[:, o + 15:o + n:16], AF.Sign, 0.0, -1.0))
-        push("aH%d" % (i + K), [("oI", i), ("ou", i), ("or", i)])
-        if i == 0:
-            push("aG2", GAPS[1])
 
-    def stW(i):
-        if i != 2 * K - 1:
-            return
-        op("a", [("y", j) for j in range(K, 2 * K)], ["sh"], act(T.sh[:], T.pa[:, Q:2 * Q], AF.Sign, -7.5), "a")
-        w = T.pm[:, 128:128 + Q]
-        terms = [(w, "ID", T.GB[:, GW + GY + Q:2 * GW], ["aG1_1"])]
+    def stH(i):
+        op("a", [("u", i)], [("ou", i)], act(goes(i)[1], T.pa[:, 64:64 + SIZES[i % K]], AF.Relu), "a")
+
+    def str_(i):
+        op("a", [("l", i)], [("or", i)], act(goes(i)[2], lists("pa", i, 192), AF.Sign), "a")
+
+    def stY(i):
+        push("aH%d" % (i + K), [("oI", i), ("ou", i), ("or", i)])
+
+    def stt(i):
+        op("a", [("y", j) for j in range(K, 2 * K)], ["sh"], act(T.sh[:], T.pa[:, Q:2 * Q], AF.Sign, 0.5 - 7.5), "a")
+
+    def stw(i):
+        terms = [(T.py[:, 384:384 + Q], "ID", T.GB[:, GW + M + Q:2 * GW], GAPS[1])]
         for k in range(K):
-            c = 128 + OFF[k] // 16
-            terms += verdicts(K + k, T.pm[:, c:c + SIZES[k] // 16])
-        sums("W1", "m", terms + [(w, "N4", T.sh[:], ["sh"])])
+            c = 384 + OFF[k] // 16
+            terms += verdicts(K + k, T.py[:, c:c + SIZES[k] // 16])
+        sums("X1", "y", terms + [(T.py[:, 384:384 + Q], "N4", T.sh[:], ["sh"])])
+
+    def written(i):
+        k = i % K
+        k0 = max([0] + [x + 1 for x in WRITES if x < k])
+        return range(i - k + k0, i + 1), OFF[k0] // 16, (OFF[k] + SIZES[k] - OFF[k0]) // 16
+
+    def stc(i):
+        s = i // K
+        turns, c, q = written(i)
+        wo, rc = T["wo%d" % s][:, c:c + q], T["rc%d" % s][:, c:c + q]
+        op("v", [("l", j) for j in turns], [("rc", i)],
+           ts(rc, T.pa[:, 192 + s * Q + c:192 + s * Q + c + q], 0.0, AO.is_gt, 0.5, AO.subtract), "a")
+        if s == 0:
+            op("v", [("rc", i), "X0"], [("wo", i)], tt(wo, rc, T.X0[:, c:c + q], AO.mult))
+        else:
+            op("v", [("rc", i), "X1"], [("wo", i)], tt(wo, T.py[:, 384 + c:384 + c + q], rc, AO.mult), "y")
+        op("v", [("wo", i)], [("ou", i, 0)],
+           ts(T.ou[:, Q * s + c:Q * s + c + q], wo, 2.0, AO.mult, DUMP - 0.5, AO.add))
 
     def stT(i):
         s = i // K
-        if i % K < K - 1 or s == ST - 1:
-            return
-        turns = range(s * K, s * K + K)
-        wo, ou = T["wo%d" % s][:], T.ou[:, Q * s:Q * s + Q]
-        ls = T.DS[:, s * M + 15:s * M + M:16]
-        dk = [("DS", j) for j in turns]
-        if s == 0:
-            op("v", dk + ["W0"], [("wo", s)], tt(wo, ls, T.W0[:], AO.min))
-        else:
-            op("v", dk + ["W1"], [("wo", s)], tt(wo, T.pm[:, 128:128 + Q], ls, AO.min), "m")
-        op("v", [("wo", s), "cd"], [("wo", s)], tt(wo, wo, T.cd[:], AO.max))
-        op("v", [("wo", s)], [("ou", s, 0)], tc(ou, wo))
-        op("v", [("ou", s, 0)] + [("In", j) for j in turns], allC,
-           tc(T.C[:, 0:DUMP + W].indirect(ou), T.In[:, s * M:s * M + M]))
+        turns, c, q = written(i)
+        op("v", [("ou", i, 0)] + [("In", j) for j in turns], allC,
+           tc(T.C[:, 0:DUMP + W].indirect(T.ou[:, Q * s + c:Q * s + c + q]),
+              T.In[:, s * M + 16 * c:s * M + 16 * (c + q)]))
 
     def stC(i):
-        if i > 0:
-            return
-        for k in range(K):
-            op("v", ["gaps"], ["gg"], tc(T.GB[:, GO[k]:GO[k] + SIZES[k]], T.gaps[:, OFF[k]:OFF[k] + SIZES[k]]),
-               None, True)
-        for h in range(2):
-            push("aG1_%d" % h, ["gg", "gy", "gw"] + [("gr", k) for k in range(K)])
+        op("v", ["gaps"], ["gg"], tc(T.GB[:, 0:M], T.gaps[:]))
+        for sname in GAPS[1]:
+            push(sname, ["gg", "gy", "gr"])
 
     def stO():
         turns = range(2 * K, 3 * K)
-        op("v", [("DS", i) for i in turns], ["y1"], ts(T.y1[:], T.DS[:, 2 * M + 15:3 * M:16], 1.0, AO.min))
+        op("v", [("l", i) for i in turns], ["y1"],
+           ts(T.y1[:], T.pa[:, 192 + 2 * Q:192 + 3 * Q], 0.0, AO.is_gt, 1.0, AO.add), "a")
         op("v", ["y1"] + [("y", i) for i in turns], ["y2"], tt(T.y2[:], T.pa[:, 2 * Q:3 * Q], T.y1[:], AO.add), "a")
         op("v", ["y2"], ["y3"], ts(T.y3[:], T.y2[:], float(B), AO.is_ge, -float(B), AO.mult))
         op("v", ["y2", "y3"], ["oFy"], tt(T.oF[:, M:M + Q], T.y2[:], T.y3[:], AO.add))
         push("aF%d" % (K - 1), ["oFy", ("oI", LAST)])
 
-    stages = {"J": stJ, "D": stD, "N": stN, "R": stR, "E": stE, "F": stF, "Y": stY, "T": stT, "C": stC, "O": stO,
-              "I": stI, "H": stH, "t": stW, "q": stQ,
-              "L": stL, "P": stP, "S": stS, "U": stU, "G": stG, "Z": stZ,
-              "A": lambda i, a: stV(i, a, 0), "B": lambda i, a: stV(i, a, 1),
-              "n": lambda i, a: stX(i, a, 0, False), "o": lambda i, a: stX(i, a, 1, False),
-              "x": lambda i, a: stX(i, a, 0, True), "w": lambda i, a: stX(i, a, 1, True)}
+    stages = {"J": lambda i: first(i, "v"), "j": lambda i: first(i, "a"), "L": stL,
+              "P": lambda i, a: running("P", i, a, "P", "A"), "n": lambda i, a: stX(i, a, False),
+              "x": lambda i, a: stX(i, a, True), "A": stA, "S": lambda i, a: running("S", i, a, "S", "V"), "U": stU,
+              "G": stG, "Z": lambda i, a: running("Z", i, a, "Z", "BB"), "D": stD, "d": std, "N": stN, "M": stM,
+              "u": stu, "R": stR, "I": stI, "E": stE, "e": ste, "l": stl, "F": stF, "h": sth, "H": stH, "r": str_,
+              "Y": stY, "t": stt, "w": stw, "c": stc, "T": stT, "C": stC, "g": lambda i: push("aG2", GAPS[1]),
+              "O": stO}
     for t in tokens(rank):
         stages[t[0]](*[int(x) for x in t[1:].split(".") if x])
 

@@ -13,20 +13,29 @@ CB = 2 * BIG
 LAST = ST * K - 1
 PIECE = 32
 XB = 4
+FREE = ST * M // PIECE % XB
 WIDE = {}
 SHARE = [("L", 1), ("G", 17)]
-PER = 1
-WRITES = [K - 1]
+PER = 3
+WRITES = [2]
+SCANNED = [8]
+GAPFIRST = 1
+LAFTER = 0
+GAPON = "v"
+ON = {"H": "a", "r": "v", "d": "a"}
 
-_R = ("P1.0 j2 G0.0 S0.1 U0.1 J2 x1.0 u0 P1.1 G0.1 D1 Z0.0 r-1 C1 A1.0 t0 g-1 Z0.1 H-1 Y-1 x1.1 N1 d1 I0 E0 w0 R0 S1.0 M1 "
-      "e0 L2.0 l0 U1.0 A1.1 F0 c0 n2.0 T0 L2.1 h0 n2.1")
+_R = ("b-1 n1.0 T-1 P1.0 n1.1 H-1 S0.1 G0.0 r-1 U0.1 x1.0 u0 G0.1 P1.1 Z0.0 D1 x1.1 d1 A1.0 N1 Z0.1 I0 S1.0 R0 E0 L2.0 "
+      "L2.1 e0 A1.1 m0 f0 Y-1 U1.0 k0 F0 M1 P2.0 G1.0 S1.1 l0 n2.0 x2.0 r0 n2.1 U1.1 P2.1 u1 D2 Z1.0 A2.0 G1.1 Z1.1 S2.0 "
+      "h0 x2.1 H0 d2 I1 M2 R1 N2 L3.0 Y0 U2.0 E1 A2.1 e1 L3.1 g0 f1 m1 S2.1 k1 l1 U2.1 h1 F1 n3.0 G2.0 P3.0 x3.0 P3.1 r1 "
+      "n3.1 u2 D3 G2.1 A3.0 Z2.0 H1 Z2.1 x3.1 t2 d3 R2 w2 I2 E2 L4.0 S3.0 e2 A3.1 m2 l2 Y1 f2 L4.1 U3.0 N3 c2 k2 a2 M3 "
+      "h2 F2")
 ROUND = {False: _R, True: _R}
-HEAD = ("L0.1 J1 L0.0 L1.0 P0.0 P0.1 C0 n0.0 P1.0 n0.1 j2 x0.0 A0.0 S0.0 U0.0 R0 x0.1 A0.1 j1 n1.0 N0 S0.1 U0.1 L1.1 P1.1 "
-        "x1.0 J2 A1.0 n1.1 N1 G0.0 Z0.0 x1.1 S1.0 G0.1 Z0.1 I0 E0 e0 U1.0 l0 A1.1 F0 L2.0 P2.0 h0 n2.0 L2.1 S1.1 N2 U1.1 "
-        "P2.1 G1.0 Z1.0 H0 r0 R1 x2.0 n2.1 A2.0 S2.0 G1.1 Z1.1 I1 E1 x2.1 A2.1 U2.0 e1 l1 Y0 L3.0 g0 F1 n3.0")
-TAIL = ("x7.1 A7.0 Z6.1 S7.0 H5 I6 Y5 A7.1 d7 L8.0 L8.1 E6 N7 P8.0 M7 R6 n8.0 U7.0 G7.0 S7.1 u7 U7.1 P8.1 e6 F6 G7.1 x8.0 "
-        "n8.1 A8.0 Z7.0 x8.1 S8.0 N8 A8.1 U8.0 D8 Z7.1 S8.1 I7 d8 U8.1 M8 E7 e7 G8.1 G8.0 Z8.0 R7 Z8.1 F7 l7 I8 E8 l6 e8 "
-        "u8 l8 R8 F8 O")
+HEAD = ("L0.0 j1 L0.1 P0.0 n0.0 C0 J1 P0.1 L1.0 R1 x0.0 A0.0 L1.1 S0.0 n0.1 U0.0 G0.0 x0.1 N1 A0.1 P1.0 S0.1 U0.1 n1.0 "
+        "N0 x1.0 G0.1 J2 P1.1 n1.1 Z0.0 A1.0 Z0.1 x1.1 I0 R0 E0 S1.0 U1.0 e0 m0 f0 k0 j2 F0 A1.1 N2 L2.0 h0 G1.0 n2.0 l0 "
+        "L2.1 P2.0 S1.1 U1.1 r0 G1.1 Z1.0 x2.0 P2.1 n2.1 A2.0 x2.1 Z1.1 S2.0 H0 Y0 L3.0 I1")
+TAIL = ("M7 e6 Y5 n8.0 A7.1 D8 P8.0 x8.0 U7.0 m6 G7.0 f6 S7.1 k6 F6 d8 U7.1 P8.1 u7 n8.1 A8.0 Z7.0 S8.0 x8.1 A8.1 M8 "
+        "G7.1 U8.0 Z7.1 S8.1 G8.0 N8 I7 l6 U8.1 E7 G8.1 Z8.0 R7 Z8.1 e7 f7 I8 m7 E8 k7 F7 u8 l7 o7 R8 e8 l8 o8 m8 p8 f8 "
+        "q8 k8 O")
 
 
 def exists(stage, i, a):
@@ -34,8 +43,9 @@ def exists(stage, i, a):
     if not 0 <= i <= LAST or a * WIDE.get(stage, 1) * PIECE >= SIZES[k]:
         return False
     return {"J": 0 < i < K, "j": 0 < i < K, "C": i == 0, "g": i == 0, "t": i == 2 * K - 1, "w": i == 2 * K - 1,
-            "c": k in WRITES and s < 2, "T": k in WRITES and s < 2}.get(
-        stage, s > 0 if stage in "DdMu" else s < 2 if stage in "hHrY" else True)
+            "o": i == LAST or (i == LAST - 1 and LAST in SCANNED), "p": i == LAST, "q": i == LAST, "F": i < LAST}.get(
+        stage, s > 0 if stage in "DdMu" else s < 2 if stage in "hHrY" else k in WRITES and s < 2 if stage in "cabT"
+        else True)
 
 
 def order(stages):
@@ -67,6 +77,9 @@ SCRATCH = {
     "RM": ("sbuf", [128, 16 * NM], "bfloat16"),
     "HB": ("sbuf", [128, 2 * NM], "float16"),
     "UW": ("sbuf", [128, 144], "float16"),
+    "MK": ("sbuf", [128, NM], "float16"),
+    "i4": ("sbuf", [128, NM], "int32"),
+    "DS": ("sbuf", [128, ST * M], "float16"),
     "i2": ("sbuf", [128, 144], "int32"),
     "i3": ("sbuf", [128, 128], "int32"),
     "I0": ("sbuf", [128, M], "float16"),
@@ -246,6 +259,10 @@ def rank_program(g, core, T, topo):
     def act(out, in_, fn, bias=0.0):
         return lambda: sc.activation(out, in_, fn, bias=bias)
 
+    def sign(stage, R, Wk, out, in_, at, bank):
+        op(ON[stage], R, Wk, act(out, in_, AF.Sign, -at) if ON[stage] == "a" else
+           ts(out, in_, at, AO.is_gt, 0.5, AO.subtract), bank)
+
     def sums(key, bank, terms, start=True, stop=True):
         for j, (out, wt, rhs, R) in enumerate(terms):
             first, last = start and j == 0, stop and j == len(terms) - 1
@@ -259,9 +276,10 @@ def rank_program(g, core, T, topo):
     for k in range(K):
         a, b = 8 * OFF[k], 8 * (OFF[k] + SIZES[k])
         load(g.sync, ("C", k), "lck%d" % k, T.C[:, DUMP + a:DUMP + b], T.ck[:, a:b])
-        if k == 0:
+        if k == LAFTER:
             load(g.sync, "L", "lla", T.L[:], T.la[:])
-    load(g.sync, "gaps", "lgap", T.gaps[:], T.gap[:])
+        if k == GAPFIRST:
+            load(g.sync, "gaps", "lgap", T.gaps[:], T.gap[:])
     allC = [("C", k) for k in range(K)]
 
     def first(k, q):
@@ -280,8 +298,10 @@ def rank_program(g, core, T, topo):
     op("v", [], ["RM"], lambda: v.memset(T.RM[:, 0:16 * NM:16], 0.0))
     op("v", ["i5", "i6"], ["b8"], tt(T.b8[:], T.i5[:], T.i6[:], AO.add))
     op("v", ["i5"], ["pm"], ts(T.pm[:], T.i5[:], -1.0 / B, AO.mult, 15.0, AO.add))
-    for name, wt in (("ID", 1.0), ("NI", -BIG), ("PI", BIG), ("NG", -1.0), ("N4", -4.0), ("HF", 0.5)):
-        op("v", ["i2"], [name], ts(T[name][:], T.i2[:, 0:128], 0.0, AO.is_equal, wt, AO.mult))
+    op("v", ["i2"], ["ID"], ts(T.ID[:], T.i2[:, 0:128], 0.0, AO.is_equal))
+    for name, wt in (("NI", -BIG), ("PI", BIG), ("NG", -1.0), ("N4", -4.0 if ON["d"] == "a" else -8.0),
+                     ("HF", 0.5 if ON["r"] == "a" else 1.0)):
+        op("a", ["ID"], [name], lambda: sc.activation(T[name][:], T.ID[:], AF.Copy, scale=wt))
     op("v", ["b8", "cus"], ["I0f"], tt(T.I0f[:], T.b8[:], T.cus[:], AO.add))
     op("v", ["cus"], ["i7"], ts(T.i7[:], T.cus[:], 1.0, AO.add))
     for k in range(K):
@@ -298,6 +318,10 @@ def rank_program(g, core, T, topo):
     half = (H - 0.5) * CB / BIG
     op("v", ["i2"], ["HB0"], ts(T.HB[:, 0:NM], T.i2[:, 0:NM], 0.0, AO.mult, -half, AO.add))
     op("v", ["i2"], ["HB1"], ts(T.HB[:, NM:2 * NM], T.i2[:, 0:NM], 0.0, AO.mult, half, AO.add))
+    if SCANNED:
+        op("v", ["i2"], ["i4"], ts(T.i4[:], T.i2[:, 0:NM], 15, AO.bitwise_and))
+        op("v", ["i4"], ["MK"], ts(T.MK[:], T.i4[:], 0.0, AO.is_gt, -40.0, AO.mult))
+        op("v", ["MK"], ["MK"], ts(T.MK[:], T.MK[:], -half, AO.add))
     op("v", ["I0f"], ["X0"], ts(T.X0[:], T.I0f[:], 0.5, AO.add))
     op("v", ["cus"], ["gy"], tc(T.GB[:, M:M + Q], T.cus[:]))
     op("v", ["I0f"], ["gr"], ts(T.GB[:, M + Q:GW], T.I0f[:], -3.0, AO.add))
@@ -394,7 +418,7 @@ def rank_program(g, core, T, topo):
         sums(("y", i), "a", [(y, "ID", ahead(i, 0), GAPS[i // K])] + verdicts(i, y))
 
     def std(i):
-        op("a", [("y", i)], [("sg", i)], act(lists("sg", i), lists("pa", i), AF.Sign, i // K / 2 - 6.5), "a")
+        sign("d", [("y", i)], [("sg", i)], lists("sg", i), lists("pa", i), 6.5 - i // K / 2, "a")
 
     def nbank(i):
         return 512 * (i % 2), ("n", i % 2)
@@ -438,30 +462,55 @@ def rank_program(g, core, T, topo):
         op("v", [("In", i), ("N", i)], [("GE", i)],
            tt(cols("GE", i), cols("In", i), T.pn[:, x + n:x + 2 * n], AO.is_ge), b)
 
+    def ybank(i):
+        return ("x", FREE) if i == LAST else "y"
+
+    def yb(i, a, b):
+        return T.px[:, 512 * FREE + a:512 * FREE + b] if i == LAST else T.py[:, a:b]
+
     def ste(i):
         s, k, n, q, o = turn(i)
         GE, gk = cols("GE", i), [("GE", i)]
-        sums(("+", i), "y", [(T.py[:, 0:2 * n], "PI", T.HB[:, NM - n:NM + n], ["HB0", "HB1"]),
-                             (T.py[:, 0:n], "BP", GE, gk), (T.py[:, n:2 * n], "BN", GE, gk)])
+        terms = [(yb(i, 0, 2 * n), "PI", T.HB[:, NM - n:NM + n], ["HB0", "HB1"])]
+        if i in SCANNED:
+            terms += [(yb(i, 256, 256 + n), "PI", T.MK[:, 0:n], ["MK"]), (yb(i, 256, 256 + n), "BP", GE, gk)]
+        sums(("+", i), ybank(i), terms + [(yb(i, 0, n), "BP", GE, gk), (yb(i, n, 2 * n), "BN", GE, gk)])
+
+    def listed(i, c, q):
+        s = i // K
+        if i in SCANNED:
+            return T.DS[:, s * M + 16 * c + 15:s * M + 16 * (c + q):16], None
+        return T.pa[:, 192 + s * Q + c:192 + s * Q + c + q], "a"
 
     def stl(i):
         s, k, n, q, o = turn(i)
+        if i in SCANNED:
+            op("v", [("+", i), "RM"], [("l", i)], lambda: v.tensor_tensor_scan(
+                cols("DS", i), T.RM[:, 0:n], yb(i, 256, 256 + n), 0.0, AO.mult, AO.max), ybank(i))
+            return
         out = lists("pa", i, 192)
         sums(("l", i), "a", [(out, "PI", T.HB[:, 0:q], ["HB0"])] +
              [(out, ("UW", 15 - e), T.GE[:, o + e:o + n:16], [("GE", i)]) for e in range(16)])
 
-    def stF(i):
+    def stf(i):
+        n = SIZES[i % K]
+        op("v", [("+", i), ("RR", i)], [("m1", i)], tt(yb(i, 2 * n, 3 * n), yb(i, 0, n), cols("RR", i), AO.min), ybank(i))
+
+    def stm(i):
+        n = SIZES[i % K]
+        op("v", [("+", i), ("In", i)], [("m2", i)], tt(cols("m2", i), yb(i, n, 2 * n), cols("In", i), AO.min), ybank(i))
+
+    def stk(i):
         s, k, n, q, o = turn(i)
         out = goes(i)[0] if s < ST - 1 else T.oF[:, OFF[k]:OFF[k] + n]
-        m1 = T.py[:, 2 * n:3 * n]
-        op("v", [("+", i), ("RR", i)], [("m1", i)], tt(m1, T.py[:, 0:n], cols("RR", i), AO.min), "y")
-        op("v", [("+", i), ("In", i)], [("m2", i)], tt(cols("m2", i), T.py[:, n:2 * n], cols("In", i), AO.min), "y")
-        op("v", [("m1", i), ("m2", i)], [("oI", i)], tt(out, m1, cols("m2", i), AO.max), "y")
-        if s < ST - 1:
-            op("v", [("oI", i)], [("oJ", i)], tc(cols("oJ", i + K), out))
+        op("v", [("m1", i), ("m2", i)], [("oI", i)], tt(out, yb(i, 2 * n, 3 * n), cols("m2", i), AO.max), ybank(i))
+
+    def stF(i):
+        if i < 2 * K:
+            op("v", [("oI", i)], [("oJ", i)], tc(cols("oJ", i + K), goes(i)[0]))
             push("aJ%d" % (i + K), [("oJ", i)])
-        elif i < LAST:
-            push("aF%d" % k, [("oI", i)])
+        else:
+            push("aF%d" % (i % K), [("oI", i)])
 
     def sth(i):
         s, k, n, q, o = turn(i)
@@ -472,16 +521,18 @@ def rank_program(g, core, T, topo):
         sums(("u", i), "a", terms + [(u, "ID", cols("m2", i), [("m2", i)])])
 
     def stH(i):
-        op("a", [("u", i)], [("ou", i)], act(goes(i)[1], T.pa[:, 64:64 + SIZES[i % K]], AF.Relu), "a")
+        out, u = goes(i)[1], T.pa[:, 64:64 + SIZES[i % K]]
+        op(ON["H"], [("u", i)], [("ou", i)], act(out, u, AF.Relu) if ON["H"] == "a" else ts(out, u, 0.0, AO.max), "a")
 
     def str_(i):
-        op("a", [("l", i)], [("or", i)], act(goes(i)[2], lists("pa", i, 192), AF.Sign), "a")
+        src, b = listed(i, OFF[i % K] // 16, SIZES[i % K] // 16)
+        sign("r", [("l", i)], [("or", i)], goes(i)[2], src, 1.0, b)
 
     def stY(i):
         push("aH%d" % (i + K), [("oI", i), ("ou", i), ("or", i)])
 
     def stt(i):
-        op("a", [("y", j) for j in range(K, 2 * K)], ["sh"], act(T.sh[:], T.pa[:, Q:2 * Q], AF.Sign, 0.5 - 7.5), "a")
+        sign("d", [("y", j) for j in range(K, 2 * K)], ["sh"], T.sh[:], T.pa[:, Q:2 * Q], 7.5 - 0.5, "a")
 
     def stw(i):
         terms = [(T.py[:, 384:384 + Q], "ID", T.GB[:, GW + M + Q:2 * GW], GAPS[1])]
@@ -495,18 +546,20 @@ def rank_program(g, core, T, topo):
         k0 = max([0] + [x + 1 for x in WRITES if x < k])
         return range(i - k + k0, i + 1), OFF[k0] // 16, (OFF[k] + SIZES[k] - OFF[k0]) // 16
 
-    def stc(i):
+    def stc(i, part):
         s = i // K
         turns, c, q = written(i)
         wo, rc = T["wo%d" % s][:, c:c + q], T["rc%d" % s][:, c:c + q]
-        op("v", [("l", j) for j in turns], [("rc", i)],
-           ts(rc, T.pa[:, 192 + s * Q + c:192 + s * Q + c + q], 0.0, AO.is_gt, 0.5, AO.subtract), "a")
-        if s == 0:
+        src, b = listed(i, c, q)
+        if part == 0:
+            op("v", [("l", j) for j in turns], [("rc", i)], ts(rc, src, 0.0, AO.is_gt, 0.5, AO.subtract), b)
+        elif part == 2:
+            op("v", [("wo", i)], [("ou", i, 0)],
+               ts(T.ou[:, Q * s + c:Q * s + c + q], wo, 2.0, AO.mult, DUMP - 0.5, AO.add))
+        elif s == 0:
             op("v", [("rc", i), "X0"], [("wo", i)], tt(wo, rc, T.X0[:, c:c + q], AO.mult))
         else:
             op("v", [("rc", i), "X1"], [("wo", i)], tt(wo, T.py[:, 384 + c:384 + c + q], rc, AO.mult), "y")
-        op("v", [("wo", i)], [("ou", i, 0)],
-           ts(T.ou[:, Q * s + c:Q * s + c + q], wo, 2.0, AO.mult, DUMP - 0.5, AO.add))
 
     def stT(i):
         s = i // K
@@ -516,16 +569,26 @@ def rank_program(g, core, T, topo):
               T.In[:, s * M + 16 * c:s * M + 16 * (c + q)]))
 
     def stC(i):
-        op("v", ["gaps"], ["gg"], tc(T.GB[:, 0:M], T.gaps[:]))
+        op(GAPON, ["gaps"], ["gg"], tc(T.GB[:, 0:M], T.gaps[:]) if GAPON == "v" else act(T.GB[:, 0:M], T.gaps[:], AF.Copy))
         for sname in GAPS[1]:
             push(sname, ["gg", "gy", "gr"])
 
-    def stO():
+    def sto(i):
+        c0 = OFF[K - 1] // 16 if i == LAST and LAST in SCANNED else 0
+        c1 = (OFF[i % K] + SIZES[i % K]) // 16
+        src, b = listed(i, c0, c1 - c0)
+        op("v", [("l", j) for j in range(2 * K, i + 1)], [("y1", i)],
+           ts(T.y1[:, c0:c1], src, 0.0, AO.is_gt, 1.0, AO.add), b)
+
+    def stp(i):
         turns = range(2 * K, 3 * K)
-        op("v", [("l", i) for i in turns], ["y1"],
-           ts(T.y1[:], T.pa[:, 192 + 2 * Q:192 + 3 * Q], 0.0, AO.is_gt, 1.0, AO.add), "a")
-        op("v", ["y1"] + [("y", i) for i in turns], ["y2"], tt(T.y2[:], T.pa[:, 2 * Q:3 * Q], T.y1[:], AO.add), "a")
+        op("v", [("y1", j) for j in turns if exists("o", j, 0)] + [("y", j) for j in turns], ["y2"],
+           tt(T.y2[:], T.pa[:, 2 * Q:3 * Q], T.y1[:], AO.add), "a")
+
+    def stq(i):
         op("v", ["y2"], ["y3"], ts(T.y3[:], T.y2[:], float(B), AO.is_ge, -float(B), AO.mult))
+
+    def stO():
         op("v", ["y2", "y3"], ["oFy"], tt(T.oF[:, M:M + Q], T.y2[:], T.y3[:], AO.add))
         push("aF%d" % (K - 1), ["oFy", ("oI", LAST)])
 
@@ -534,8 +597,9 @@ def rank_program(g, core, T, topo):
               "x": lambda i, a: stX(i, a, True), "A": stA, "S": lambda i, a: running("S", i, a, "S", "V"), "U": stU,
               "G": stG, "Z": lambda i, a: running("Z", i, a, "Z", "BB"), "D": stD, "d": std, "N": stN, "M": stM,
               "u": stu, "R": stR, "I": stI, "E": stE, "e": ste, "l": stl, "F": stF, "h": sth, "H": stH, "r": str_,
-              "Y": stY, "t": stt, "w": stw, "c": stc, "T": stT, "C": stC, "g": lambda i: push("aG2", GAPS[1]),
-              "O": stO}
+              "Y": stY, "t": stt, "w": stw, "T": stT, "C": stC, "g": lambda i: push("aG2", GAPS[1]),
+              "c": lambda i: stc(i, 0), "a": lambda i: stc(i, 1), "b": lambda i: stc(i, 2),
+              "f": stf, "m": stm, "k": stk, "o": sto, "p": stp, "q": stq, "O": stO}
     for t in tokens(rank):
         stages[t[0]](*[int(x) for x in t[1:].split(".") if x])
 

from concourse.mybir import AluOpType, ActivationFunctionType

M, B, H, ST, W = 192, 8, 5, 3, 1536
SIZES = [64, 64, 64]
K = len(SIZES)
OFF = [sum(SIZES[:k]) for k in range(K)]
NM = max(SIZES)
Q = M // 16
QS = 2 * -(-NM // 32)
DUMP = W + 8
BIG = 2048.0
CB = 2 * BIG
LAST = ST * K - 1
PIECE = 32
XB = 4
FREE = ST * M // PIECE % XB
WIDE = {}
SHARE = [("L", 1), ("G", 17)]
PER = 3
WRITES = [2]
SCANNED = [8]
GAPFIRST = 1
LAFTER = 0
GAPON = "v"
ON = {"H": "a", "r": "v", "d": "a"}

_R = ("b-1 n1.0 T-1 P1.0 n1.1 H-1 S0.1 G0.0 r-1 U0.1 x1.0 u0 G0.1 P1.1 Z0.0 D1 x1.1 d1 A1.0 N1 Z0.1 I0 S1.0 R0 E0 L2.0 "
      "L2.1 e0 A1.1 m0 f0 Y-1 U1.0 k0 F0 M1 P2.0 G1.0 S1.1 l0 n2.0 x2.0 r0 n2.1 U1.1 P2.1 u1 D2 Z1.0 A2.0 G1.1 Z1.1 S2.0 "
      "h0 x2.1 H0 d2 I1 M2 R1 N2 L3.0 Y0 U2.0 E1 A2.1 e1 L3.1 g0 f1 m1 S2.1 k1 l1 U2.1 h1 F1 n3.0 G2.0 P3.0 x3.0 P3.1 r1 "
      "n3.1 u2 D3 G2.1 A3.0 Z2.0 H1 Z2.1 x3.1 t2 d3 R2 w2 I2 E2 L4.0 S3.0 e2 A3.1 m2 l2 Y1 f2 L4.1 U3.0 N3 c2 k2 a2 M3 "
      "h2 F2")
ROUND = {False: _R, True: _R}
HEAD = ("L0.0 j1 L0.1 P0.0 n0.0 C0 J1 P0.1 L1.0 R1 x0.0 A0.0 L1.1 S0.0 n0.1 U0.0 G0.0 x0.1 N1 A0.1 P1.0 S0.1 U0.1 n1.0 "
        "N0 x1.0 G0.1 J2 P1.1 n1.1 Z0.0 A1.0 Z0.1 x1.1 I0 R0 E0 S1.0 U1.0 e0 m0 f0 k0 j2 F0 A1.1 N2 L2.0 h0 G1.0 n2.0 l0 "
        "L2.1 P2.0 S1.1 U1.1 r0 G1.1 Z1.0 x2.0 P2.1 n2.1 A2.0 x2.1 Z1.1 S2.0 H0 Y0 L3.0 I1")
TAIL = ("M7 e6 Y5 n8.0 A7.1 D8 P8.0 x8.0 U7.0 m6 G7.0 f6 S7.1 k6 F6 d8 U7.1 P8.1 u7 n8.1 A8.0 Z7.0 S8.0 x8.1 A8.1 M8 "
        "G7.1 U8.0 Z7.1 S8.1 G8.0 N8 I7 l6 U8.1 E7 G8.1 Z8.0 R7 Z8.1 e7 f7 I8 m7 E8 k7 F7 u8 l7 o7 R8 e8 l8 o8 m8 p8 f8 "
        "q8 k8 O")


def exists(stage, i, a):
    s, k = divmod(i, K)
    if not 0 <= i <= LAST or a * WIDE.get(stage, 1) * PIECE >= SIZES[k]:
        return False
    return {"J": 0 < i < K, "j": 0 < i < K, "C": i == 0, "g": i == 0, "t": i == 2 * K - 1, "w": i == 2 * K - 1,
            "o": i == LAST or (i == LAST - 1 and LAST in SCANNED), "p": i == LAST, "q": i == LAST, "F": i < LAST}.get(
        stage, s > 0 if stage in "DdMu" else s < 2 if stage in "hHrY" else k in WRITES and s < 2 if stage in "cabT"
        else True)


def order(stages):
    out = []
    for t in range(-4 * PER, LAST + 4 * PER, PER):
        for x in stages.split():
            i, dot, a = x[1:].partition(".")
            if exists(x[0], t + int(i), int(a or 0)):
                out.append(x[0] + str(t + int(i)) + dot + a)
    head, tail = HEAD.split(), TAIL.split()
    return head + [t for t in out if t not in head and t not in tail] + tail


ORDERS = {r: order(ROUND[r]) for r in ROUND}


def pad8(x):
    return -(-x // 8) * 8


GW = M + 2 * Q
HO = [sum(pad8(4 * n + n // 8) for n in SIZES[:k]) for k in range(K + 1)]
SCRATCH = {
    "C": ("sbuf", [128, DUMP + W], "int32"),
    "L": ("sbuf", [128, W], "int32"),
    "cus": ("sbuf", [128, Q], "int32"),
    "gaps": ("sbuf", [128, M], "int32"),
    "GB": ("sbuf", [128, ST * GW], "float16"),
    "RM": ("sbuf", [128, 16 * NM], "bfloat16"),
    "HB": ("sbuf", [128, 2 * NM], "float16"),
    "UW": ("sbuf", [128, 144], "float16"),
    "MK": ("sbuf", [128, NM], "float16"),
    "i4": ("sbuf", [128, NM], "int32"),
    "DS": ("sbuf", [128, ST * M], "float16"),
    "i2": ("sbuf", [128, 144], "int32"),
    "i3": ("sbuf", [128, 128], "int32"),
    "I0": ("sbuf", [128, M], "float16"),
    "Ru": ("sbuf", [128, ST * K * QS], "uint16"),
    "sg": ("sbuf", [128, ST * Q], "float16"),
    "sh": ("sbuf", [128, Q], "float16"),
    "ou": ("sbuf", [128, ST * Q], "uint16"),
    "I0u": ("sbuf", [128, K * QS], "uint16"),
    "J": ("sbuf", [128, ST * M], "uint16"),
    "oJ": ("sbuf", [128, ST * M], "uint16"),
    "oH": ("sbuf", [128, HO[K]], "float16"),
    "H1": ("sbuf", [128, HO[K]], "float16"),
    "H2": ("sbuf", [128, HO[K]], "float16"),
    "oF": ("sbuf", [128, M + Q], "float32"),
    "px": ("psum", [128, XB * 512], "float32"),
    "pn": ("psum", [128, 2 * 512], "float32"),
    "py": ("psum", [128, 512], "float32"),
    "pa": ("psum", [128, 512], "float32"),
}
for _k in range(K):
    SCRATCH["F%d" % _k] = ("dram", [128, SIZES[_k] + Q * (_k == K - 1)], "float32")
for _n in ("ID", "NG", "NI", "PI", "N4", "HF", "BP", "BN"):
    SCRATCH[_n] = ("sbuf", [128, 128], "float16")
for _n in ("i5", "i6", "i7"):
    SCRATCH[_n] = ("sbuf", [128, Q], "int32")
for _n in ("b8", "pm", "I0f", "R0f", "X0", "rc0", "rc1", "wo0", "wo1", "y1", "y2", "y3"):
    SCRATCH[_n] = ("sbuf", [128, Q], "float32")
for _n in ("A", "V", "P", "S", "BB", "Z"):
    SCRATCH[_n] = ("sbuf", [128, ST * M * 16], "float16")
for _n, _d in (("su", "uint16"), ("RR", "float16"), ("In", "float16"), ("GE", "float16"), ("m2", "float16")):
    SCRATCH[_n] = ("sbuf", [128, ST * M], _d)
SEMAPHORES = ["v", "a", "p", "gq", "ls", "lcu", "lla", "lgap", "st", "aG1_0", "aG1_1", "aG2"]
SEMAPHORES += ["lck%d" % _k for _k in range(K)]
SEMAPHORES += ["a%s%d" % (_n, _i) for _n in "JH" for _i in range(K, ST * K)] + ["aF%d" % _k for _k in range(K)]

GH = pad8(GW // 2)
MSG = {"aG1_0": ("GB", GW, GH, "GB", 0, 0), "aG1_1": ("GB", GW + GH, GW - GH, "GB", GH, 1),
       "aG2": ("GB", 2 * GW, GW, "GB", GW, 1)}
GAPS = [["gg"], ["aG1_0", "aG1_1"], ["aG2"]]
for _k in range(K):
    _n, _q = SIZES[_k], SIZES[_k] // 16
    for _s in (1, 2):
        MSG["aJ%d" % (_s * K + _k)] = ("J", _s * M + OFF[_k], _n, "oJ", _s * M + OFF[_k], 0)
    MSG["aH%d" % (K + _k)] = ("H1", HO[_k], 2 * _n + _q, "oH", HO[_k], 1)
    MSG["aH%d" % (2 * K + _k)] = ("H2", HO[_k], 2 * _n + 2 * _q, "H1", HO[_k] + 2 * _n, 1)
    MSG["aF%d" % _k] = ("F%d" % _k, 0, _n + Q * (_k == K - 1), "oF", OFF[_k], 0)


def issue(tokens):
    out = []
    for t in tokens:
        i = int(t[1:]) if t[0] in "FY" else None
        if t[0] == "C":
            out += GAPS[1]
        elif t[0] == "g":
            out += GAPS[2]
        elif t[0] == "F" and i < LAST:
            out.append("aJ%d" % (i + K) if i < 2 * K else "aF%d" % (i - 2 * K))
        elif t[0] == "Y":
            out.append("aH%d" % (i + K))
        elif t == "O":
            out.append("aF%d" % (K - 1))
    return out


def lanes(topo, cores, src, dst):
    if topo.may_write(src, dst):
        return [dst, dst]
    own = [c for c in topo.cores_of(src) if c not in cores and topo.may_write(c, dst)]
    own.sort(key=lambda c: (topo.die(c) != topo.die(src), c))
    return [own[0], own[1 % len(own)]]


def nbits(m):
    return bin(m).count("1")


def rank_program(g, core, T, topo):
    cores = list(T.cores)
    n_ranks = len(cores)
    sem = T.sem
    rank = T.rank_of(core)

    def tokens(r):
        return ORDERS[not topo.may_write(cores[(r - 1) % n_ranks], cores[r])]

    def send(dst, sname, relay):
        name, c, n, src, cs = MSG[sname][:5]
        if relay:
            src, cs = name, c
        rid, pid = topo.addr(dst, core)
        m = topo.mask(core, dst)
        g.remote_dma(T[name][:, c:c + n], T[src][:, cs:cs + n], sem[sname], sem.ls, pid, rid, m)
        return nbits(m)

    if rank is None:
        total = 0
        for r in range(n_ranks):
            src, dst = cores[r], cores[(r + 1) % n_ranks]
            way = lanes(topo, cores, src, dst)
            if core not in way:
                continue
            for sname in issue(tokens(r)):
                if way[MSG[sname][5]] == core:
                    g.wait_ge(sem[sname], nbits(topo.mask(src, core)))
                    total += send(dst, sname, True)
        if total:
            g.wait_ge(sem.ls, total)
        return

    nxt, prv = cores[(rank + 1) % n_ranks], cores[(rank - 1) % n_ranks]
    way = lanes(topo, cores, core, nxt)
    inway = lanes(topo, cores, prv, core)
    arrives = [nbits(topo.mask(prv if w == core else w, core)) for w in inway]
    sent = [0]

    queues = {"v": (g.vector, "v"), "a": (g.scalar, "a"), "p": (g.tensor, "p"), "g": (g, "gq"), "s": (g.sync, "st")}
    count = {q: 0 for q in queues}
    seen = {q: {} for q in queues}
    wrote, readers, banks = {}, {}, {}

    def wait(q, deps):
        need = {}
        for s, val in deps:
            need[s] = max(need.get(s, 0), val)
        for s in sorted(need):
            if seen[q].get(s, 0) < need[s]:
                queues[q][0].wait_ge(sem[s], need[s])
                seen[q][s] = need[s]

    def op(q, R, Wk, call, bank=None, group=False):
        d = [wrote[k] for k in R]
        for k in Wk:
            if k in wrote and not group:
                d.append(wrote[k])
            d += readers.get(k, [])
        if bank is not None:
            d += [t for qq, t in banks.get(bank, {}).items() if qq != q]
        wait(q, d)
        s = queues[q][1]
        call().then_inc(sem[s], 1)
        count[q] += 1
        tok = (s, count[q])
        for k in R:
            readers.setdefault(k, []).append(tok)
        for k in Wk:
            wrote[k] = tok
            readers[k] = []
        if bank is not None:
            banks.setdefault(bank, {})[q] = tok

    def load(eng, name, s, out, in_):
        eng.dma_start(out, in_).then_inc(sem[s], 16)
        wrote[name] = (s, 16)

    def push(sname, R):
        wait("g", [wrote[k] for k in R])
        sent[0] += send(way[MSG[sname][5]], sname, False)

    for sname in MSG:
        wrote[sname] = (sname, arrives[MSG[sname][5]])

    AO, AF = AluOpType, ActivationFunctionType
    v, te, sc = g.vector, g.tensor, g.scalar

    def ts(out, in0, s1, o0, s2=None, o1=None):
        if o1 is None:
            return lambda: v.tensor_scalar(out, in0, s1, None, o0)
        return lambda: v.tensor_scalar(out, in0, s1, s2, o0, o1)

    def tt(out, a, b, o):
        return lambda: v.tensor_tensor(out, a, b, o)

    def tc(out, in_):
        return lambda: v.tensor_copy(out, in_)

    def act(out, in_, fn, bias=0.0):
        return lambda: sc.activation(out, in_, fn, bias=bias)

    def sign(stage, R, Wk, out, in_, at, bank):
        op(ON[stage], R, Wk, act(out, in_, AF.Sign, -at) if ON[stage] == "a" else
           ts(out, in_, at, AO.is_gt, 0.5, AO.subtract), bank)

    def sums(key, bank, terms, start=True, stop=True):
        for j, (out, wt, rhs, R) in enumerate(terms):
            first, last = start and j == 0, stop and j == len(terms) - 1
            name, c = wt if isinstance(wt, tuple) else (wt, 0)
            op("p", R + [name], [key], lambda: te.matmul(out, T[name][:, c:c + 128], rhs, first, last), bank, not first)

    def gather(q, R, Wk, out, win, off):
        op(q, R, Wk, tc(out, win.indirect(off)) if q == "v" else lambda: sc.activation(out, win.indirect(off), AF.Copy))

    load(g.scalar, "cus", "lcu", T.cus[:], T.cu[:])
    for k in range(K):
        a, b = 8 * OFF[k], 8 * (OFF[k] + SIZES[k])
        load(g.sync, ("C", k), "lck%d" % k, T.C[:, DUMP + a:DUMP + b], T.ck[:, a:b])
        if k == LAFTER:
            load(g.sync, "L", "lla", T.L[:], T.la[:])
        if k == GAPFIRST:
            load(g.sync, "gaps", "lgap", T.gaps[:], T.gap[:])
    allC = [("C", k) for k in range(K)]

    def first(k, q):
        o, n = OFF[k], SIZES[k]
        name = "J" if q == "v" else "I0"
        gather(q, [("I0u", k)] + allC[:k + 1], [(name, k)], T[name][:, o:o + n], T.C[:, DUMP:DUMP + 8 * (o + n)],
               T.I0u[:, QS * k:QS * k + n // 16])

    op("g", [], ["i5"], lambda: g.iota(T.i5[:], [[0, Q]], 0, 8))
    op("g", [], ["i6"], lambda: g.iota(T.i6[:], [[128, Q]], 0, 0))
    op("g", [], ["i2"], lambda: g.iota(T.i2[:], [[1, 144]], 0, -1))
    op("g", [], ["i3"], lambda: g.iota(T.i3[:], [[16, 8], [0, 16]], 15, -1))

    op("v", [], ["RM"], lambda: v.memset(T.RM[:], 1.0))
    op("v", ["i5"], ["i5"], ts(T.i5[:], T.i5[:], 127, AO.bitwise_and))
    op("v", [], ["RM"], lambda: v.memset(T.RM[:, 0:16 * NM:16], 0.0))
    op("v", ["i5", "i6"], ["b8"], tt(T.b8[:], T.i5[:], T.i6[:], AO.add))
    op("v", ["i5"], ["pm"], ts(T.pm[:], T.i5[:], -1.0 / B, AO.mult, 15.0, AO.add))
    op("v", ["i2"], ["ID"], ts(T.ID[:], T.i2[:, 0:128], 0.0, AO.is_equal))
    for name, wt in (("NI", -BIG), ("PI", BIG), ("NG", -1.0), ("N4", -4.0 if ON["d"] == "a" else -8.0),
                     ("HF", 0.5 if ON["r"] == "a" else 1.0)):
        op("a", ["ID"], [name], lambda: sc.activation(T[name][:], T.ID[:], AF.Copy, scale=wt))
    op("v", ["b8", "cus"], ["I0f"], tt(T.I0f[:], T.b8[:], T.cus[:], AO.add))
    op("v", ["cus"], ["i7"], ts(T.i7[:], T.cus[:], 1.0, AO.add))
    for k in range(K):
        c, q = OFF[k] // 16, SIZES[k] // 16
        op("v", ["I0f"], [("I0u", k)], tc(T.I0u[:, QS * k:QS * k + q], T.I0f[:, c:c + q]))
    op("v", ["i7"], ["i7"], ts(T.i7[:], T.i7[:], B - 1, AO.bitwise_and))
    op("v", ["i3"], ["i3"], ts(T.i3[:], T.i3[:], 4, AO.arith_shift_right))
    first(0, "v")
    first(0, "a")
    op("v", ["b8", "i7"], ["R0f"], tt(T.R0f[:], T.b8[:], T.i7[:], AO.add))
    op("v", ["i3"], ["BP"], ts(T.BP[:], T.i3[:], 0.0, AO.is_equal, CB, AO.mult))
    op("v", ["i3"], ["BN"], ts(T.BN[:], T.i3[:], 0.0, AO.is_equal, -CB, AO.mult))
    op("v", ["i2", "pm"], ["UW"], ts(T.UW[:], T.i2[:], T.pm[:, 0:1], AO.is_equal, CB, AO.mult))
    half = (H - 0.5) * CB / BIG
    op("v", ["i2"], ["HB0"], ts(T.HB[:, 0:NM], T.i2[:, 0:NM], 0.0, AO.mult, -half, AO.add))
    op("v", ["i2"], ["HB1"], ts(T.HB[:, NM:2 * NM], T.i2[:, 0:NM], 0.0, AO.mult, half, AO.add))
    if SCANNED:
        op("v", ["i2"], ["i4"], ts(T.i4[:], T.i2[:, 0:NM], 15, AO.bitwise_and))
        op("v", ["i4"], ["MK"], ts(T.MK[:], T.i4[:], 0.0, AO.is_gt, -40.0, AO.mult))
        op("v", ["MK"], ["MK"], ts(T.MK[:], T.MK[:], -half, AO.add))
    op("v", ["I0f"], ["X0"], ts(T.X0[:], T.I0f[:], 0.5, AO.add))
    op("v", ["cus"], ["gy"], tc(T.GB[:, M:M + Q], T.cus[:]))
    op("v", ["I0f"], ["gr"], ts(T.GB[:, M + Q:GW], T.I0f[:], -3.0, AO.add))
    for k in range(K):
        c, q = OFF[k] // 16, SIZES[k] // 16
        op("v", ["R0f"], [("Ru", k)], tc(T.Ru[:, QS * k:QS * k + q], T.R0f[:, c:c + q]))

    def turn(i):
        s, k = divmod(i, K)
        return s, k, SIZES[k], SIZES[k] // 16, s * M + OFF[k]

    def cols(name, i):
        s, k, n, q, o = turn(i)
        return T[name][:, o:o + n]

    def lists(name, i, at=0):
        s, k, n, q, o = turn(i)
        return T[name][:, at + o // 16:at + o // 16 + q]

    def came(i, a, b):
        s, k, n, q, o = turn(i)
        if s == 0:
            return T.I0[:, o + a:o + b]
        h = HO[k] + (s - 1) * q
        return (T.H1 if s == 1 else T.H2)[:, h + a:h + b]

    def camekey(i):
        return [("I0", i) if i < K else "aH%d" % i]

    def goes(i):
        s, k, n, q, o = turn(i)
        buf, h = (T.oH, HO[k]) if s == 0 else (T.H1, HO[k] + 2 * n + q)
        return buf[:, h:h + n], buf[:, h + n:h + 2 * n], buf[:, h + 2 * n:h + 2 * n + q]

    def span(stage, i, a):
        s, k, n, q, o = turn(i)
        w = WIDE.get(stage, 1) * PIECE
        w, o = min(w, n - a * w), o + a * w
        return o, w, range(o // PIECE, (o + w) // PIECE)

    def wide(name, o, w):
        return T[name][:, 16 * o:16 * (o + w)]

    def ends(name, o, w):
        return T[name][:, 16 * o + 15:16 * (o + w):16]

    def keys(name, js):
        return [(name, j) for j in js]

    def gathers(stage, i, a, R, out, win, lst):
        o, w, js = span(stage, i, a)
        gather("v" if (stage, js[0]) in SHARE else "a", R, keys(out, js), wide(out, o, w), win, lst[:, o:o + w])

    def running(stage, i, a, out, src):
        o, w, js = span(stage, i, a)
        op("v", keys(src, js) + ["RM"], keys(out, js),
           lambda: v.tensor_tensor_scan(wide(out, o, w), T.RM[:, 0:16 * w], wide(src, o, w), 0.0, AO.mult, AO.max))

    def stL(i, a):
        gathers("L", i, a, [("J", i) if i < K else "aJ%d" % i, "L"], "A", T.L[:], T.J)

    def stX(i, a, tops):
        o, w, (j,) = span("A", i, a)
        b, x = ("x", j % XB), 512 * (j % XB)
        if not tops:
            sums(("X", j), b, [(T.px[:, x:x + 512], "NI", wide("A", o, w), [("A", j)])], stop=False)
        else:
            sums(("X", j), b, [(T.px[:, x + e:x + 512:16], "PI", ends("P", o, w), [("P", j)]) for e in range(16)],
                 start=False)

    def stA(i, a):
        o, w, (j,) = span("A", i, a)
        b, x = ("x", j % XB), 512 * (j % XB)
        op("v", [("A", j), ("X", j)], [("V", j)], tt(wide("V", o, w), T.px[:, x:x + 512], wide("A", o, w), AO.min), b)

    def stU(i, a):
        o, w, js = span("U", i, a)
        op("v", keys("S", js), keys("su", js), tc(T.su[:, o:o + w], ends("S", o, w)))

    def stG(i, a):
        gathers("G", i, a, keys("su", span("G", i, a)[2]) + allC, "BB", T.C[:, DUMP:DUMP + W], T.su)

    def verdicts(i, out):
        s, k, n, q, o = turn(i)
        return [(out, "HF", came(i, a, a + q), camekey(i)) for a in (2 * n, -q)[:s]]

    def ahead(i, part):
        s, k, n, q, o = turn(i)
        c = s * GW + M + part * Q + OFF[k] // 16
        return T.GB[:, c:c + q]

    def stD(i):
        y = lists("pa", i)
        sums(("y", i), "a", [(y, "ID", ahead(i, 0), GAPS[i // K])] + verdicts(i, y))

    def std(i):
        sign("d", [("y", i)], [("sg", i)], lists("sg", i), lists("pa", i), 6.5 - i // K / 2, "a")

    def nbank(i):
        return 512 * (i % 2), ("n", i % 2)

    def stN(i):
        s, k, n, q, o = turn(i)
        I, hk = came(i, 0, n), camekey(i)
        x, b = nbank(i)
        bound = T.pn[:, x + n:x + 2 * n]
        terms = [(T.pn[:, x:x + n], "ID", I, hk), (bound, "ID", I, hk),
                 (bound, "ID", T.GB[:, s * GW + OFF[k]:s * GW + OFF[k] + n], GAPS[s])]
        if s > 0:
            terms.append((bound, "NG", came(i, n, 2 * n), hk))
        sums(("N", i), b, terms)

    def stM(i):
        s, k, n, q, o = turn(i)
        x, b = nbank(i)
        lst = T.pn[:, x + 256:x + 256 + q]
        sums(("M", i), b, [(lst, "ID", ahead(i, 1), GAPS[s])] + verdicts(i, lst) +
             [(lst, "N4", lists("sg", i), [("sg", i)])])

    def stu(i):
        s, k, n, q, o = turn(i)
        x, b = nbank(i)
        op("v", [("M", i)], [("Ru", i)], ts(T.Ru[:, QS * i:QS * i + q], T.pn[:, x + 256:x + 256 + q], s / 2, AO.add), b)

    def stR(i):
        s, k, n, q, o = turn(i)
        gather("v" if ("R", i) in SHARE else "a", [("Ru", i)] + allC, [("RR", i)], cols("RR", i), T.C[:, DUMP:DUMP + W], T.Ru[:, QS * i:QS * i + q])

    def stI(i):
        s, k, n, q, o = turn(i)
        x, b = nbank(i)
        zk = keys("Z", range(o // PIECE, (o + n) // PIECE))
        op("v", zk + [("N", i)], [("In", i)], tt(cols("In", i), T.pn[:, x:x + n], ends("Z", o, n), AO.max), b)

    def stE(i):
        s, k, n, q, o = turn(i)
        x, b = nbank(i)
        op("v", [("In", i), ("N", i)], [("GE", i)],
           tt(cols("GE", i), cols("In", i), T.pn[:, x + n:x + 2 * n], AO.is_ge), b)

    def ybank(i):
        return ("x", FREE) if i == LAST else "y"

    def yb(i, a, b):
        return T.px[:, 512 * FREE + a:512 * FREE + b] if i == LAST else T.py[:, a:b]

    def ste(i):
        s, k, n, q, o = turn(i)
        GE, gk = cols("GE", i), [("GE", i)]
        terms = [(yb(i, 0, 2 * n), "PI", T.HB[:, NM - n:NM + n], ["HB0", "HB1"])]
        if i in SCANNED:
            terms += [(yb(i, 256, 256 + n), "PI", T.MK[:, 0:n], ["MK"]), (yb(i, 256, 256 + n), "BP", GE, gk)]
        sums(("+", i), ybank(i), terms + [(yb(i, 0, n), "BP", GE, gk), (yb(i, n, 2 * n), "BN", GE, gk)])

    def listed(i, c, q):
        s = i // K
        if i in SCANNED:
            return T.DS[:, s * M + 16 * c + 15:s * M + 16 * (c + q):16], None
        return T.pa[:, 192 + s * Q + c:192 + s * Q + c + q], "a"

    def stl(i):
        s, k, n, q, o = turn(i)
        if i in SCANNED:
            op("v", [("+", i), "RM"], [("l", i)], lambda: v.tensor_tensor_scan(
                cols("DS", i), T.RM[:, 0:n], yb(i, 256, 256 + n), 0.0, AO.mult, AO.max), ybank(i))
            return
        out = lists("pa", i, 192)
        sums(("l", i), "a", [(out, "PI", T.HB[:, 0:q], ["HB0"])] +
             [(out, ("UW", 15 - e), T.GE[:, o + e:o + n:16], [("GE", i)]) for e in range(16)])

    def stf(i):
        n = SIZES[i % K]
        op("v", [("+", i), ("RR", i)], [("m1", i)], tt(yb(i, 2 * n, 3 * n), yb(i, 0, n), cols("RR", i), AO.min), ybank(i))

    def stm(i):
        n = SIZES[i % K]
        op("v", [("+", i), ("In", i)], [("m2", i)], tt(cols("m2", i), yb(i, n, 2 * n), cols("In", i), AO.min), ybank(i))

    def stk(i):
        s, k, n, q, o = turn(i)
        out = goes(i)[0] if s < ST - 1 else T.oF[:, OFF[k]:OFF[k] + n]
        op("v", [("m1", i), ("m2", i)], [("oI", i)], tt(out, yb(i, 2 * n, 3 * n), cols("m2", i), AO.max), ybank(i))

    def stF(i):
        if i < 2 * K:
            op("v", [("oI", i)], [("oJ", i)], tc(cols("oJ", i + K), goes(i)[0]))
            push("aJ%d" % (i + K), [("oJ", i)])
        else:
            push("aF%d" % (i % K), [("oI", i)])

    def sth(i):
        s, k, n, q, o = turn(i)
        u, hk = T.pa[:, 64:64 + n], camekey(i)
        terms = [(u, "NG", came(i, 0, n), hk)]
        if s > 0:
            terms.append((u, "ID", came(i, n, 2 * n), hk))
        sums(("u", i), "a", terms + [(u, "ID", cols("m2", i), [("m2", i)])])

    def stH(i):
        out, u = goes(i)[1], T.pa[:, 64:64 + SIZES[i % K]]
        op(ON["H"], [("u", i)], [("ou", i)], act(out, u, AF.Relu) if ON["H"] == "a" else ts(out, u, 0.0, AO.max), "a")

    def str_(i):
        src, b = listed(i, OFF[i % K] // 16, SIZES[i % K] // 16)
        sign("r", [("l", i)], [("or", i)], goes(i)[2], src, 1.0, b)

    def stY(i):
        push("aH%d" % (i + K), [("oI", i), ("ou", i), ("or", i)])

    def stt(i):
        sign("d", [("y", j) for j in range(K, 2 * K)], ["sh"], T.sh[:], T.pa[:, Q:2 * Q], 7.5 - 0.5, "a")

    def stw(i):
        terms = [(T.py[:, 384:384 + Q], "ID", T.GB[:, GW + M + Q:2 * GW], GAPS[1])]
        for k in range(K):
            c = 384 + OFF[k] // 16
            terms += verdicts(K + k, T.py[:, c:c + SIZES[k] // 16])
        sums("X1", "y", terms + [(T.py[:, 384:384 + Q], "N4", T.sh[:], ["sh"])])

    def written(i):
        k = i % K
        k0 = max([0] + [x + 1 for x in WRITES if x < k])
        return range(i - k + k0, i + 1), OFF[k0] // 16, (OFF[k] + SIZES[k] - OFF[k0]) // 16

    def stc(i, part):
        s = i // K
        turns, c, q = written(i)
        wo, rc = T["wo%d" % s][:, c:c + q], T["rc%d" % s][:, c:c + q]
        src, b = listed(i, c, q)
        if part == 0:
            op("v", [("l", j) for j in turns], [("rc", i)], ts(rc, src, 0.0, AO.is_gt, 0.5, AO.subtract), b)
        elif part == 2:
            op("v", [("wo", i)], [("ou", i, 0)],
               ts(T.ou[:, Q * s + c:Q * s + c + q], wo, 2.0, AO.mult, DUMP - 0.5, AO.add))
        elif s == 0:
            op("v", [("rc", i), "X0"], [("wo", i)], tt(wo, rc, T.X0[:, c:c + q], AO.mult))
        else:
            op("v", [("rc", i), "X1"], [("wo", i)], tt(wo, T.py[:, 384 + c:384 + c + q], rc, AO.mult), "y")

    def stT(i):
        s = i // K
        turns, c, q = written(i)
        op("v", [("ou", i, 0)] + [("In", j) for j in turns], allC,
           tc(T.C[:, 0:DUMP + W].indirect(T.ou[:, Q * s + c:Q * s + c + q]),
              T.In[:, s * M + 16 * c:s * M + 16 * (c + q)]))

    def stC(i):
        op(GAPON, ["gaps"], ["gg"], tc(T.GB[:, 0:M], T.gaps[:]) if GAPON == "v" else act(T.GB[:, 0:M], T.gaps[:], AF.Copy))
        for sname in GAPS[1]:
            push(sname, ["gg", "gy", "gr"])

    def sto(i):
        c0 = OFF[K - 1] // 16 if i == LAST and LAST in SCANNED else 0
        c1 = (OFF[i % K] + SIZES[i % K]) // 16
        src, b = listed(i, c0, c1 - c0)
        op("v", [("l", j) for j in range(2 * K, i + 1)], [("y1", i)],
           ts(T.y1[:, c0:c1], src, 0.0, AO.is_gt, 1.0, AO.add), b)

    def stp(i):
        turns = range(2 * K, 3 * K)
        op("v", [("y1", j) for j in turns if exists("o", j, 0)] + [("y", j) for j in turns], ["y2"],
           tt(T.y2[:], T.pa[:, 2 * Q:3 * Q], T.y1[:], AO.add), "a")

    def stq(i):
        op("v", ["y2"], ["y3"], ts(T.y3[:], T.y2[:], float(B), AO.is_ge, -float(B), AO.mult))

    def stO():
        op("v", ["y2", "y3"], ["oFy"], tt(T.oF[:, M:M + Q], T.y2[:], T.y3[:], AO.add))
        push("aF%d" % (K - 1), ["oFy", ("oI", LAST)])

    stages = {"J": lambda i: first(i, "v"), "j": lambda i: first(i, "a"), "L": stL,
              "P": lambda i, a: running("P", i, a, "P", "A"), "n": lambda i, a: stX(i, a, False),
              "x": lambda i, a: stX(i, a, True), "A": stA, "S": lambda i, a: running("S", i, a, "S", "V"), "U": stU,
              "G": stG, "Z": lambda i, a: running("Z", i, a, "Z", "BB"), "D": stD, "d": std, "N": stN, "M": stM,
              "u": stu, "R": stR, "I": stI, "E": stE, "e": ste, "l": stl, "F": stF, "h": sth, "H": stH, "r": str_,
              "Y": stY, "t": stt, "w": stw, "T": stT, "C": stC, "g": lambda i: push("aG2", GAPS[1]),
              "c": lambda i: stc(i, 0), "a": lambda i: stc(i, 1), "b": lambda i: stc(i, 2),
              "f": stf, "m": stm, "k": stk, "o": sto, "p": stp, "q": stq, "O": stO}
    for t in tokens(rank):
        stages[t[0]](*[int(x) for x in t[1:].split(".") if x])

    total = 0
    for k in range(K):
        wait("s", [wrote["aF%d" % k]])
        g.sync.dma_start(T.yi[:, OFF[k]:OFF[k] + SIZES[k]], T["F%d" % k][:, 0:SIZES[k]]).then_inc(sem.st, 16)
        total += 16
    wait("a", [wrote["aF%d" % (K - 1)]])
    g.scalar.dma_start(T.yc[:], T["F%d" % (K - 1)][:, SIZES[-1]:SIZES[-1] + Q]).then_inc(sem.st, 16)
    total += 16
    g.sync.wait_ge(sem.st, total)
    g.wait_ge(sem.ls, sent[0])
    for q, s in (("v", "v"), ("a", "a"), ("p", "p"), ("g", "gq")):
        g.wait_ge(sem[s], count[q])
